import numpy as np
import ml_dtypes


def mxq(x, axis, fmt="e4m3"):
    dtype, down = {"e4m3": (ml_dtypes.float8_e4m3fn, 7), "e5m2": (ml_dtypes.float8_e5m2, 14)}[fmt]
    v = np.moveaxis(np.asarray(x, np.float32).astype(ml_dtypes.bfloat16).astype(np.float64), axis, -1)
    blocks = v.reshape(v.shape[:-1] + (-1, 32))
    amax = np.abs(blocks).max(-1, keepdims=True)
    byte = np.maximum(np.where(amax > 0, np.frexp(amax)[1] - 1 + 127, 0) - down, 1)
    scale = np.exp2(byte - 127.0)
    codes = (blocks / scale).astype(np.float32).astype(dtype).astype(np.float64)
    return np.moveaxis((codes * scale).reshape(v.shape), -1, axis)


WIDE = False


def mx_kscale(k):
    if not WIDE:
        return np.ones(k)
    levels = np.array([10, -10, 5, -5, 0])
    if k % 512:
        return np.exp2(np.random.permutation(np.resize(levels, k // 32))).repeat(32)
    a = np.empty((k // 512, 16))
    for p in range(k // 512):
        a[p, :8] = np.random.permutation(np.resize(levels, 8))
        for g in range(8):
            far = levels[np.abs(levels - a[p, g]) >= 10]
            a[p, g + 8] = far[np.random.randint(len(far))]
    return np.exp2(a.ravel()).repeat(32)


def f64(x):
    return np.asarray(x).astype(np.float64)


def striped(idx):
    return np.tile(idx.reshape(-1, 16).T, (8, 1)).astype(np.uint16)


def unstriped(offs):
    return offs[:16].T.reshape(-1).astype(np.int64)


E2M1 = np.array([0.0, 0.5, 1.0, 1.5, 2.0, 3.0, 4.0, 6.0, -0.0, -0.5, -1.0, -1.5, -2.0, -3.0, -4.0, -6.0])


def pack_weight(w, fmt):
    k, n = w.shape
    w = f64(np.asarray(w, np.float32).astype(ml_dtypes.bfloat16)).reshape(k // 32, 32, n)
    amax = np.abs(w).max(1)
    if fmt == "e4m3":
        byte = np.frexp(amax)[1] - 1 + 127 - 7
    else:
        mant, ex = np.frexp(amax / 6.0)
        byte = np.where(mant > 0.5, ex, ex - 1) + 127
    byte = np.clip(np.where(amax > 0, byte, 1), 1, 254)
    scaled = (w * np.exp2(127.0 - byte)[:, None, :]).reshape(k, n).astype(np.float32)
    by_word = np.ascontiguousarray(scaled.reshape(k // 512, 128, 4, n).transpose(0, 1, 3, 2))
    if fmt == "e4m3":
        words = by_word.astype(ml_dtypes.float8_e4m3fn).view(np.uint8)
    else:
        c = by_word.astype(ml_dtypes.float4_e2m1fn).view(np.uint8) & 0xF
        words = (c[..., 0::2] | (c[..., 1::2] << 4)).reshape(k // 512, 128, 2 * n)
    return np.ascontiguousarray(words), np.ascontiguousarray(byte.astype(np.uint8).reshape(k // 512, 16, n))


def unpack_weight(words, scales, fmt):
    g, _, n = scales.shape
    words = np.ascontiguousarray(words).reshape(g, 128, n, -1)
    if fmt == "e4m3":
        vals = words.view(ml_dtypes.float8_e4m3fn).astype(np.float64)
    else:
        nib = np.empty((g, 128, n, 4), np.uint8)
        nib[..., 0::2] = words & 0xF
        nib[..., 1::2] = words >> 4
        vals = E2M1[nib]
    vals = vals * np.repeat(np.exp2(scales.astype(np.float64) - 127.0), 8, axis=1)[..., None]
    return vals.transpose(0, 1, 3, 2).reshape(g * 512, n)


def pack_table(v):
    words, scales = pack_weight(v, "e4m3")
    return np.concatenate([words.reshape(words.shape[0], -1), scales.reshape(scales.shape[0], -1)], axis=1)


def unpack_table(tab):
    g, t = tab.shape[0], tab.shape[1] // 528
    return unpack_weight(tab[:, :512 * t].reshape(g, 128, t, 4), tab[:, 512 * t:].reshape(g, 16, t), "e4m3")


K, R, M, T, S = 1536, 512, 1024, 4096, 1536


def setup_inputs():
    n = np.random.standard_normal
    s = mx_kscale(K)[:, None]
    u = mx_kscale(R)[:, None]
    p_w4 = pack_weight(n((K, M)) / np.sqrt(K) / s, "e2m1")
    return {
        "tab": pack_table(n((K, T)) * s),
        "w4_words": p_w4[0],
        "w4_scales": p_w4[1],
        "down": (n((K, R)) / np.sqrt(K) / s * u.T).astype(np.float32),
        "up": (0.5 * n((R, M)) / np.sqrt(R) / u).astype(np.float32),
        "prev": (n((1024, 1536))).astype(np.float32),
        "offs": striped(np.random.permutation(T)[:S]),
    }


def reference(tab, w4_words, w4_scales, down, up, prev, offs):
    tab_ = unpack_table(tab)[:, unstriped(offs)]
    w4_ = unpack_weight(w4_words, w4_scales, "e2m1")
    down_ = mxq(f64(down), 0, "e4m3")
    up_ = mxq(f64(up), 0, "e4m3")
    h_ = mxq(down_.T @ tab_, 0, "e4m3")
    y = w4_.T @ tab_ + up_.T @ h_
    return f64(prev) + y

@@ -1,0 +1,269 @@
+from contextlib import ExitStack
+
+import concourse.mybir as mybir
+
+K, R, M, T, S = 1536, 512, 1024, 4096, 1536
+
+FLOPS = 2 * S * (K * R + K * M + R * M)
+
+F32 = mybir.dt.float32
+BF16 = mybir.dt.bfloat16
+I32 = mybir.dt.int32
+U32 = mybir.dt.uint32
+U16 = mybir.dt.uint16
+U8 = mybir.dt.uint8
+FP8X4 = mybir.dt.float8_e4m3fn_x4
+FP4X4 = mybir.dt.float4_e2m1fn_x4
+ADD = mybir.AluOpType.add
+
+P = 128
+PASSES = K // 512
+NT = 512
+CHUNKS = S // NT
+RT = R // P
+MT = M // P
+
+
+def tile_list_tablora_res_kernel(
+    tc, tab, w4_words, w4_scales, down, up, prev, offs, out
+):
+    nc = tc.nc
+    with ExitStack() as ctx:
+        lists = ctx.enter_context(tc.tile_pool(name="lists", bufs=1))
+        keep = ctx.enter_context(tc.tile_pool(name="keep", bufs=1))
+        raws = ctx.enter_context(tc.tile_pool(name="raws", bufs=3))
+        grps = ctx.enter_context(tc.tile_pool(name="grps", bufs=3))
+        hbs = ctx.enter_context(tc.tile_pool(name="hbs", bufs=2))
+        psum = ctx.enter_context(tc.psum_pool(name="psum", bufs=8))
+
+        offsets = lists.tile([P, S // 16], U16, name="offsets")
+        nc.sync.dma_start(offsets[:], offs)
+
+        raw = [raws.tile([P, 4, R], F32, name="raw") for a in range(PASSES)]
+        win_w = [keep.tile([P, T], I32, name=f"win_w{a}", align_bytes=64) for a in range(PASSES)]
+        win_s = keep.tile([P, T // 4], I32, name="win_s", align_bytes=64)
+        w4w = keep.tile([P, PASSES, 2 * M], U8, name="w4w", align_bytes=64)
+        w4s = keep.tile([P, PASSES, M], U8, name="w4s", align_bytes=64)
+        up_raw = keep.tile([P, 4, M], F32, name="up_raw")
+        res = keep.tile([P, MT, S], F32, name="res")
+        moved = [keep.tile([P, S], U8, name=f"moved{a}", align_bytes=64) for a in range(1, PASSES)]
+
+        def load_pass(a):
+            nc.sync.dma_start(out=raw[a][:], in_=down[512 * a : 512 * (a + 1), :].rearrange("(p j) w -> p j w", j=4))
+            nc.sync.dma_start(
+                out=win_w[a][:], in_=tab[a, 0 : 512 * T].rearrange("(p b) -> p b", p=P).bitcast(I32)
+            )
+
+        load_pass(0)
+        nc.vector.memset(win_s[:], 0)
+        rows = tab[:, 512 * T : 528 * T].rearrange("a (q t) -> a q t", q=16).bitcast(I32)
+        for q in range(4):
+            nc.gpsimd.dma_start(out=win_s[32 * q : 32 * q + 12, :], in_=rows[:, 4 * q : 4 * q + 4, :])
+        nc.gpsimd.memset(w4s[:].rearrange("p a n -> p (a n)").bitcast(I32), 0)
+        for t in moved:
+            nc.gpsimd.memset(t[:].bitcast(I32), 0)
+        nc.gpsimd.memset(raw[1][:, 0, 0:1], 0.0)
+        nc.gpsimd.memset(win_w[1][:, 0:1], 0)
+        nc.gpsimd.memset(raw[2][:, 0, 0:1], 0.0)
+        nc.gpsimd.memset(win_w[2][:, 0:1], 0)
+        nc.gpsimd.memset(w4w[:, 0, :].bitcast(I32)[:, 0:1], 0)
+
+        load_pass(1)
+        load_pass(2)
+        nc.sync.dma_start(
+            out=w4w[:].bitcast(I32), in_=w4_words.bitcast(I32).rearrange("a p b -> p a b")
+        )
+        w4s_rows = w4_scales.bitcast(I32)
+        for q in range(4):
+            nc.gpsimd.dma_start(
+                out=w4s[32 * q : 32 * q + 4, :, :].bitcast(I32),
+                in_=w4s_rows[:, 4 * q : 4 * q + 4, :].rearrange("a r n -> r a n"),
+            )
+
+        dcodes, dscales = [], []
+
+        def quantize_down(a):
+            grp = grps.tile([P, 4 * R], BF16, name="grp", align_bytes=64)
+            dst = grp[:].rearrange("p (t m j) -> p m t j", t=4, j=4)
+            src = raw[a][:].rearrange("p j (m t) -> p m t j", t=4)
+            m0 = P if a < PASSES - 1 else P // 2
+            nc.scalar.copy(out=dst[:, :m0, :, :], in_=src[:, :m0, :, :])
+            if m0 < P:
+                nc.vector.tensor_copy(out=dst[:, m0:, :, :], in_=src[:, m0:, :, :])
+            c = keep.tile([P, R], U32, name=f"dcodes{a}", align_bytes=64)
+            s = keep.tile([P, R], U8, name=f"dscales{a}", align_bytes=64)
+            nc.vector.quantize_mx(out=c[:].bitcast(FP8X4), scales=s[:], in_=grp[:])
+            dcodes.append(c)
+            dscales.append(s)
+
+        gs = keep.tile([P, S], U8, name="gs", align_bytes=64)
+        gw = {}
+        OC = NT // 16
+
+        def gather_scales(n):
+            nc.vector.tensor_copy(
+                gs[:, NT * n : NT * (n + 1)],
+                win_s[:].bitcast(U8).indirect(offsets[:, OC * n : OC * (n + 1)]),
+            )
+
+        def gather_words(a, n):
+            t = keep.tile([P, NT], U32, name=f"gw{a}_{n}", align_bytes=64)
+            nc.vector.tensor_copy(
+                t[:], win_w[a][:].bitcast(U32).indirect(offsets[:, OC * n : OC * (n + 1)])
+            )
+            gw[a, n] = t
+
+        def open_bank():
+            return psum.tile([P, NT], F32, name="bank")
+
+        LAST = CHUNKS - 1
+
+        def h_pass(bank, a, n, t, start, stop):
+            nc.tensor.matmul_mx(
+                out=bank[:],
+                lhsT=dcodes[a][:, P * t : P * (t + 1)].bitcast(FP8X4),
+                lhsT_scale=dscales[a][:, P * t : P * (t + 1)],
+                rhs=gw[a, n][:].bitcast(FP8X4),
+                rhs_scale=gs[4 * a : P, NT * n : NT * (n + 1)],
+                start=start,
+                stop=stop,
+            )
+
+        def h_last(bank, a, b, t, start, stop):
+            nc.tensor.matmul_mx(
+                out=bank[:, P * t : P * (t + 1)],
+                lhsT=dcodes[a][:, P * t : P * (t + 1)].bitcast(FP8X4),
+                lhsT_scale=dscales[a][:, P * t : P * (t + 1)],
+                rhs=gw[a, LAST][:, P * b : P * (b + 1)].bitcast(FP8X4),
+                rhs_scale=gs[4 * a : P, NT * LAST + P * b : NT * LAST + P * (b + 1)],
+                start=start,
+                stop=stop,
+            )
+
+        quantize_down(0)
+        banks = {}
+        gather_scales(0)
+        gather_words(0, 0)
+        gather_scales(1)
+        gather_scales(2)
+        gather_words(0, 1)
+        gather_words(0, 2)
+        for t in range(RT):
+            banks[0, t] = open_bank()
+            h_pass(banks[0, t], 0, 0, t, True, False)
+        for a in range(1, PASSES):
+            for q in range(4):
+                (nc.sync if a == 1 else nc.gpsimd).dma_start(
+                    out=moved[a - 1][32 * q : 32 * q + 4, :].bitcast(I32),
+                    in_=gs[32 * q + 4 * a : 32 * q + 4 * a + 4, :].bitcast(I32),
+                )
+        nc.vector.tensor_copy(up_raw[:, 0, 0:1], raw[2][:, 0, 0:1])
+        nc.sync.dma_start(out=up_raw[:], in_=up.rearrange("(p j) w -> p j w", j=4))
+        quantize_down(1)
+        for n in (2, 0, 1):
+            gather_words(1, n)
+        part = []
+        for b in range(4):
+            bank = open_bank()
+            for t in range(RT):
+                for a in range(2):
+                    h_last(bank, a, b, t, a == 0, a == 1)
+            x = keep.tile([P, P, 4], F32, name=f"part{b}")
+            nc.scalar.copy(out=x[:], in_=bank[:].rearrange("p (t c) -> p c t", t=RT))
+            part.append(x)
+        for t in range(RT):
+            h_pass(banks[0, t], 1, 0, t, False, False)
+        for t in range(RT):
+            banks[1, t] = open_bank()
+            for a in range(2):
+                h_pass(banks[1, t], a, 1, t, a == 0, False)
+        quantize_down(2)
+        for n in range(CHUNKS):
+            gather_words(2, n)
+        hb = []
+        for n in range(LAST):
+            x = hbs.tile([P, RT, NT], BF16, name="hb")
+            hb.append(x)
+            for t in range(RT):
+                h_pass(banks[n, t], 2, n, t, False, True)
+            for t in range(RT):
+                nc.scalar.copy(out=x[:, t, :], in_=banks[n, t][:])
+        nc.vector.tensor_copy(res[:, :, 0:1], hb[0][:, 0, 0:MT].rearrange("p (m o) -> p m o", o=1))
+        for m in range(MT):
+            nc.sync.dma_start(out=res[:, m, :], in_=prev[P * m : P * (m + 1), :])
+        hcodes, hscales = [], []
+        for n in range(CHUNKS):
+            grp = grps.tile([P, 4 * R], BF16, name="grp", align_bytes=64)
+            if n < LAST:
+                nc.vector.tensor_copy(
+                    out=grp[:].rearrange("p (c i t) -> p c t i", i=4, t=4),
+                    in_=hb[n][:].rearrange("p t (c i) -> p c t i", i=4),
+                )
+            else:
+                for b in range(4):
+                    bank = open_bank()
+                    for t in range(RT):
+                        h_last(bank, 2, b, t, True, True)
+                    nc.vector.tensor_tensor(
+                        grp[:, 512 * b : 512 * (b + 1)].rearrange("p (c t) -> p c t", t=4),
+                        bank[:].rearrange("p (t c) -> p c t", t=RT),
+                        part[b][:],
+                        ADD,
+                    )
+            c = keep.tile([P, NT], U32, name=f"hcodes{n}", align_bytes=64)
+            s = keep.tile([P, NT], U8, name=f"hscales{n}", align_bytes=64)
+            nc.vector.quantize_mx(out=c[:].bitcast(FP8X4), scales=s[:], in_=grp[:])
+            hcodes.append(c)
+            hscales.append(s)
+
+        up_grp = keep.tile([P, M, 4], BF16, name="up_grp", align_bytes=64)
+        ucodes = keep.tile([P, M], U32, name="ucodes", align_bytes=64)
+        uscales = keep.tile([P, M], U8, name="uscales", align_bytes=64)
+        for i in range(4):
+            cols = slice(256 * i, 256 * (i + 1))
+            nc.scalar.copy(
+                out=up_grp[:, cols, :].rearrange("p (c i) j -> p c j i", i=4),
+                in_=up_raw[:, :, cols].rearrange("p j (c i) -> p c j i", i=4),
+            )
+            nc.vector.quantize_mx(
+                out=ucodes[:, cols].bitcast(FP8X4),
+                scales=uscales[:, cols],
+                in_=up_grp[:, cols, :].rearrange("p c j -> p (c j)"),
+            )
+
+        half = 2
+        order = [(m, n) for m in range(half) for n in range(LAST)]
+        order += [(m, LAST) for m in range(half)]
+        order += [(m, n) for m in range(half, MT) for n in range(CHUNKS)]
+        for m, n in order:
+            cols = slice(NT * n, NT * (n + 1))
+            y = open_bank()
+            for a in range(PASSES):
+                plane = gs if a == 0 else moved[a - 1]
+                nc.tensor.matmul_mx(
+                    out=y[:],
+                    lhsT=w4w[:, a, 256 * m : 256 * (m + 1)].bitcast(FP4X4),
+                    lhsT_scale=w4s[:, a, P * m : P * (m + 1)],
+                    rhs=gw[a, n][:].bitcast(FP8X4),
+                    rhs_scale=plane[:, cols],
+                    start=(a == 0),
+                    stop=False,
+                )
+            nc.tensor.matmul_mx(
+                out=y[:],
+                lhsT=ucodes[:, P * m : P * (m + 1)].bitcast(FP8X4),
+                lhsT_scale=uscales[:, P * m : P * (m + 1)],
+                rhs=hcodes[n][:].bitcast(FP8X4),
+                rhs_scale=hscales[n][:],
+                start=False,
+                stop=True,
+            )
+            halves = 2 if m == MT - 1 and n == LAST else 1
+            w = NT // halves
+            for i in range(halves):
+                part_cols = slice(NT * n + w * i, NT * n + w * (i + 1))
+                nc.vector.tensor_tensor(res[:, m, part_cols], y[:, w * i : w * (i + 1)], res[:, m, part_cols], ADD)
+                if m == MT - 1:
+                    nc.scalar.dma_start(out=out[P * m : P * (m + 1), part_cols], in_=res[:, m, part_cols])
+            if m < MT - 1 and n == LAST:
+                nc.scalar.dma_start(out=out[P * m : P * (m + 1), :], in_=res[:, m, :])

@@ -24,6 +24,10 @@ RT = R // P
 MT = M // P
 
 
+KB = 1024
+SCALE_ROWS = (16, 48, 112)
+
+
 def tile_list_tablora_res_kernel(
     tc, tab, w4_words, w4_scales, down, up, prev, offs, out
 ):
@@ -31,48 +35,43 @@ def tile_list_tablora_res_kernel(
     with ExitStack() as ctx:
         lists = ctx.enter_context(tc.tile_pool(name="lists", bufs=1))
         keep = ctx.enter_context(tc.tile_pool(name="keep", bufs=1))
-        raws = ctx.enter_context(tc.tile_pool(name="raws", bufs=3))
+        stage = ctx.enter_context(tc.tile_pool(name="stage", bufs=1))
         grps = ctx.enter_context(tc.tile_pool(name="grps", bufs=3))
-        hbs = ctx.enter_context(tc.tile_pool(name="hbs", bufs=2))
         psum = ctx.enter_context(tc.psum_pool(name="psum", bufs=8))
 
+        def staged(name, shape, dtype, kb):
+            return stage.tile(shape, dtype, name=name, offset=kb * KB, align_bytes=64)
+
+        win_s = staged("win_s", [P, T // 4], I32, 48)
+        rows = tab[:, 512 * T : 528 * T].rearrange("a (q t) -> a q t", q=16).bitcast(I32)
+        for a in (0, 2, 1):
+            nc.sync.dma_start(out=win_s[SCALE_ROWS[a] : SCALE_ROWS[a] + 16, :], in_=rows[a])
+        nc.vector.memset(win_s[0:16, :], 0)
+        nc.vector.memset(win_s[32:48, :], 0)
+        nc.vector.memset(win_s[64:112, :], 0)
         offsets = lists.tile([P, S // 16], U16, name="offsets")
         nc.sync.dma_start(offsets[:], offs)
 
-        raw = [raws.tile([P, 4, R], F32, name="raw") for a in range(PASSES)]
-        win_w = [keep.tile([P, T], I32, name=f"win_w{a}", align_bytes=64) for a in range(PASSES)]
-        win_s = keep.tile([P, T // 4], I32, name="win_s", align_bytes=64)
-        w4w = keep.tile([P, PASSES, 2 * M], U8, name="w4w", align_bytes=64)
-        w4s = keep.tile([P, PASSES, M], U8, name="w4s", align_bytes=64)
-        up_raw = keep.tile([P, 4, M], F32, name="up_raw")
-        res = keep.tile([P, MT, S], F32, name="res")
-        moved = [keep.tile([P, S], U8, name=f"moved{a}", align_bytes=64) for a in range(1, PASSES)]
+        raw, win_w = {}, {}
 
-        def load_pass(a):
+        def load_down(a):
+            raw[a] = staged(f"raw{a}", [P, 4, R], F32, (0, 42, 2)[a])
             nc.sync.dma_start(out=raw[a][:], in_=down[512 * a : 512 * (a + 1), :].rearrange("(p j) w -> p j w", j=4))
+
+        def load_words(a):
+            win_w[a] = staged(f"win_w{a}", [P, T], I32, 50 if a == 1 else 72)
             nc.sync.dma_start(
                 out=win_w[a][:], in_=tab[a, 0 : 512 * T].rearrange("(p b) -> p b", p=P).bitcast(I32)
             )
 
-        load_pass(0)
-        nc.vector.memset(win_s[:], 0)
-        rows = tab[:, 512 * T : 528 * T].rearrange("a (q t) -> a q t", q=16).bitcast(I32)
-        for q in range(4):
-            nc.gpsimd.dma_start(out=win_s[32 * q : 32 * q + 12, :], in_=rows[:, 4 * q : 4 * q + 4, :])
-        nc.gpsimd.memset(w4s[:].rearrange("p a n -> p (a n)").bitcast(I32), 0)
-        for t in moved:
-            nc.gpsimd.memset(t[:].bitcast(I32), 0)
-        nc.gpsimd.memset(raw[1][:, 0, 0:1], 0.0)
-        nc.gpsimd.memset(win_w[1][:, 0:1], 0)
-        nc.gpsimd.memset(raw[2][:, 0, 0:1], 0.0)
-        nc.gpsimd.memset(win_w[2][:, 0:1], 0)
-        nc.gpsimd.memset(w4w[:, 0, :].bitcast(I32)[:, 0:1], 0)
+        load_down(0)
+        load_words(0)
 
-        load_pass(1)
-        load_pass(2)
-        nc.sync.dma_start(
-            out=w4w[:].bitcast(I32), in_=w4_words.bitcast(I32).rearrange("a p b -> p a b")
-        )
+        w4s = keep.tile([P, PASSES, M], U8, name="w4s", align_bytes=64)
+        planes = [keep.tile([P, S], U8, name=f"plane{a}", align_bytes=64) for a in range(PASSES - 1)]
+        nc.vector.memset(w4s[:].rearrange("p a n -> p (a n)").bitcast(I32), 0)
+        for plane in planes:
+            nc.vector.memset(plane[:].bitcast(I32), 0)
         w4s_rows = w4_scales.bitcast(I32)
         for q in range(4):
             nc.gpsimd.dma_start(
@@ -80,31 +79,40 @@ def tile_list_tablora_res_kernel(
                 in_=w4s_rows[:, 4 * q : 4 * q + 4, :].rearrange("a r n -> r a n"),
             )
 
+        gs = keep.tile([P, S], U8, name="gs", align_bytes=64)
+        nc.vector.tensor_copy(gs[:], win_s[:].bitcast(U8).indirect(offsets[:]))
+
+        def move_plane(a, queue):
+            for q in range(4):
+                first = SCALE_ROWS[a] + 4 * q
+                queue.dma_start(
+                    out=planes[a][32 * q : 32 * q + 4, :].bitcast(I32),
+                    in_=gs[first : first + 4, :].bitcast(I32),
+                )
+
+        move_plane(0, nc.sync)
+        load_down(1)
+        move_plane(1, nc.sync)
+        load_words(1)
+
         dcodes, dscales = [], []
 
         def quantize_down(a):
             grp = grps.tile([P, 4 * R], BF16, name="grp", align_bytes=64)
             dst = grp[:].rearrange("p (t m j) -> p m t j", t=4, j=4)
             src = raw[a][:].rearrange("p j (m t) -> p m t j", t=4)
-            m0 = P if a < PASSES - 1 else P // 2
-            nc.scalar.copy(out=dst[:, :m0, :, :], in_=src[:, :m0, :, :])
-            if m0 < P:
-                nc.vector.tensor_copy(out=dst[:, m0:, :, :], in_=src[:, m0:, :, :])
+            if a < PASSES - 1:
+                nc.scalar.copy(out=dst, in_=src)
+            else:
+                nc.vector.tensor_copy(out=dst, in_=src)
             c = keep.tile([P, R], U32, name=f"dcodes{a}", align_bytes=64)
             s = keep.tile([P, R], U8, name=f"dscales{a}", align_bytes=64)
             nc.vector.quantize_mx(out=c[:].bitcast(FP8X4), scales=s[:], in_=grp[:])
             dcodes.append(c)
             dscales.append(s)
 
-        gs = keep.tile([P, S], U8, name="gs", align_bytes=64)
         gw = {}
         OC = NT // 16
-
-        def gather_scales(n):
-            nc.vector.tensor_copy(
-                gs[:, NT * n : NT * (n + 1)],
-                win_s[:].bitcast(U8).indirect(offsets[:, OC * n : OC * (n + 1)]),
-            )
 
         def gather_words(a, n):
             t = keep.tile([P, NT], U32, name=f"gw{a}_{n}", align_bytes=64)
@@ -118,98 +126,73 @@ def tile_list_tablora_res_kernel(
 
         LAST = CHUNKS - 1
 
-        def h_pass(bank, a, n, t, start, stop):
-            nc.tensor.matmul_mx(
-                out=bank[:],
-                lhsT=dcodes[a][:, P * t : P * (t + 1)].bitcast(FP8X4),
-                lhsT_scale=dscales[a][:, P * t : P * (t + 1)],
-                rhs=gw[a, n][:].bitcast(FP8X4),
-                rhs_scale=gs[4 * a : P, NT * n : NT * (n + 1)],
-                start=start,
-                stop=stop,
-            )
+        def h_passes(bank, a, n, b, start, stop):
+            for t in range(RT):
+                nc.tensor.matmul_mx(
+                    out=bank[:, P * t : P * (t + 1)],
+                    lhsT=dcodes[a][:, P * t : P * (t + 1)].bitcast(FP8X4),
+                    lhsT_scale=dscales[a][:, P * t : P * (t + 1)],
+                    rhs=gw[a, n][:, P * b : P * (b + 1)].bitcast(FP8X4),
+                    rhs_scale=planes[a][:, NT * n + P * b : NT * n + P * (b + 1)],
+                    start=start and t == 0,
+                    stop=stop and t == RT - 1,
+                )
 
-        def h_last(bank, a, b, t, start, stop):
-            nc.tensor.matmul_mx(
-                out=bank[:, P * t : P * (t + 1)],
-                lhsT=dcodes[a][:, P * t : P * (t + 1)].bitcast(FP8X4),
-                lhsT_scale=dscales[a][:, P * t : P * (t + 1)],
-                rhs=gw[a, LAST][:, P * b : P * (b + 1)].bitcast(FP8X4),
-                rhs_scale=gs[4 * a : P, NT * LAST + P * b : NT * LAST + P * (b + 1)],
-                start=start,
-                stop=stop,
-            )
+        def interleaved(bank):
+            return bank[:].rearrange("p (t c) -> p c t", t=RT)
 
         quantize_down(0)
+        load_down(2)
+        planes.append(staged("plane2", [P, S], U8, 0))
+        nc.vector.memset(planes[2][:].bitcast(I32), 0)
+        move_plane(2, nc.sync)
         banks = {}
-        gather_scales(0)
-        gather_words(0, 0)
-        gather_scales(1)
-        gather_scales(2)
-        gather_words(0, 1)
-        gather_words(0, 2)
-        for t in range(RT):
-            banks[0, t] = open_bank()
-            h_pass(banks[0, t], 0, 0, t, True, False)
-        for a in range(1, PASSES):
-            for q in range(4):
-                (nc.sync if a == 1 else nc.gpsimd).dma_start(
-                    out=moved[a - 1][32 * q : 32 * q + 4, :].bitcast(I32),
-                    in_=gs[32 * q + 4 * a : 32 * q + 4 * a + 4, :].bitcast(I32),
-                )
-        nc.vector.tensor_copy(up_raw[:, 0, 0:1], raw[2][:, 0, 0:1])
-        nc.sync.dma_start(out=up_raw[:], in_=up.rearrange("(p j) w -> p j w", j=4))
+        for n in (0, LAST, 1):
+            gather_words(0, n)
+        load_words(2)
+        for n in (0, LAST):
+            for b in range(4):
+                banks[n, b] = open_bank()
+                h_passes(banks[n, b], 0, n, b, True, False)
         quantize_down(1)
-        for n in (2, 0, 1):
+        for n in (LAST, 0, 1):
             gather_words(1, n)
+        w4w = staged("w4w", [P, PASSES, 2 * M], U8, 50)
+        nc.sync.dma_start(
+            out=w4w[:].bitcast(I32), in_=w4_words.bitcast(I32).rearrange("a p b -> p a b")
+        )
+        up_raw = staged("up_raw", [P, 4, M], F32, 56)
+        nc.sync.dma_start(out=up_raw[:], in_=up.rearrange("(p j) w -> p j w", j=4))
         part = []
         for b in range(4):
-            bank = open_bank()
-            for t in range(RT):
-                for a in range(2):
-                    h_last(bank, a, b, t, a == 0, a == 1)
+            h_passes(banks[LAST, b], 1, LAST, b, False, True)
             x = keep.tile([P, P, 4], F32, name=f"part{b}")
-            nc.scalar.copy(out=x[:], in_=bank[:].rearrange("p (t c) -> p c t", t=RT))
+            nc.scalar.copy(out=x[:], in_=interleaved(banks[LAST, b]))
             part.append(x)
-        for t in range(RT):
-            h_pass(banks[0, t], 1, 0, t, False, False)
-        for t in range(RT):
-            banks[1, t] = open_bank()
+        for b in range(4):
+            h_passes(banks[0, b], 1, 0, b, False, False)
+        for b in range(4):
+            banks[1, b] = open_bank()
             for a in range(2):
-                h_pass(banks[1, t], a, 1, t, a == 0, False)
+                h_passes(banks[1, b], a, 1, b, a == 0, False)
         quantize_down(2)
-        for n in range(CHUNKS):
-            gather_words(2, n)
-        hb = []
-        for n in range(LAST):
-            x = hbs.tile([P, RT, NT], BF16, name="hb")
-            hb.append(x)
-            for t in range(RT):
-                h_pass(banks[n, t], 2, n, t, False, True)
-            for t in range(RT):
-                nc.scalar.copy(out=x[:, t, :], in_=banks[n, t][:])
-        nc.vector.tensor_copy(res[:, :, 0:1], hb[0][:, 0, 0:MT].rearrange("p (m o) -> p m o", o=1))
+        res = staged("res", [P, MT, S], F32, 2)
         for m in range(MT):
             nc.sync.dma_start(out=res[:, m, :], in_=prev[P * m : P * (m + 1), :])
+        for n in range(CHUNKS):
+            gather_words(2, n)
         hcodes, hscales = [], []
         for n in range(CHUNKS):
             grp = grps.tile([P, 4 * R], BF16, name="grp", align_bytes=64)
-            if n < LAST:
-                nc.vector.tensor_copy(
-                    out=grp[:].rearrange("p (c i t) -> p c t i", i=4, t=4),
-                    in_=hb[n][:].rearrange("p t (c i) -> p c t i", i=4),
-                )
-            else:
-                for b in range(4):
+            for b in range(4):
+                dst = grp[:, 512 * b : 512 * (b + 1)].rearrange("p (c t) -> p c t", t=4)
+                if n < LAST:
+                    h_passes(banks[n, b], 2, n, b, False, True)
+                    nc.scalar.copy(out=dst, in_=interleaved(banks[n, b]))
+                else:
                     bank = open_bank()
-                    for t in range(RT):
-                        h_last(bank, 2, b, t, True, True)
-                    nc.vector.tensor_tensor(
-                        grp[:, 512 * b : 512 * (b + 1)].rearrange("p (c t) -> p c t", t=4),
-                        bank[:].rearrange("p (t c) -> p c t", t=RT),
-                        part[b][:],
-                        ADD,
-                    )
+                    h_passes(bank, 2, n, b, True, True)
+                    nc.vector.tensor_tensor(dst, interleaved(bank), part[b][:], ADD)
             c = keep.tile([P, NT], U32, name=f"hcodes{n}", align_bytes=64)
             s = keep.tile([P, NT], U8, name=f"hscales{n}", align_bytes=64)
             nc.vector.quantize_mx(out=c[:].bitcast(FP8X4), scales=s[:], in_=grp[:])
@@ -239,13 +222,12 @@ def tile_list_tablora_res_kernel(
             cols = slice(NT * n, NT * (n + 1))
             y = open_bank()
             for a in range(PASSES):
-                plane = gs if a == 0 else moved[a - 1]
                 nc.tensor.matmul_mx(
                     out=y[:],
                     lhsT=w4w[:, a, 256 * m : 256 * (m + 1)].bitcast(FP4X4),
                     lhsT_scale=w4s[:, a, P * m : P * (m + 1)],
                     rhs=gw[a, n][:].bitcast(FP8X4),
-                    rhs_scale=plane[:, cols],
+                    rhs_scale=planes[a][:, cols],
                     start=(a == 0),
                     stop=False,
                 )

@@ -42,24 +42,24 @@ def tile_list_tablora_res_kernel(
         def staged(name, shape, dtype, kb):
             return stage.tile(shape, dtype, name=name, offset=kb * KB, align_bytes=64)
 
-        win_s = staged("win_s", [P, T // 4], I32, 48)
+        win_s = staged("win_s", [P, T // 4], I32, 62)
         rows = tab[:, 512 * T : 528 * T].rearrange("a (q t) -> a q t", q=16).bitcast(I32)
         for a in (0, 2, 1):
             nc.sync.dma_start(out=win_s[SCALE_ROWS[a] : SCALE_ROWS[a] + 16, :], in_=rows[a])
         nc.vector.memset(win_s[0:16, :], 0)
-        nc.vector.memset(win_s[32:48, :], 0)
-        nc.vector.memset(win_s[64:112, :], 0)
+        nc.gpsimd.memset(win_s[32:48, :], 0)
+        nc.gpsimd.memset(win_s[64:112, :], 0)
         offsets = lists.tile([P, S // 16], U16, name="offsets")
         nc.sync.dma_start(offsets[:], offs)
 
         raw, win_w = {}, {}
 
         def load_down(a):
-            raw[a] = staged(f"raw{a}", [P, 4, R], F32, (0, 42, 2)[a])
+            raw[a] = staged(f"raw{a}", [P, 4, R], F32, (14, 56, 14)[a])
             nc.sync.dma_start(out=raw[a][:], in_=down[512 * a : 512 * (a + 1), :].rearrange("(p j) w -> p j w", j=4))
 
         def load_words(a):
-            win_w[a] = staged(f"win_w{a}", [P, T], I32, 50 if a == 1 else 72)
+            win_w[a] = staged(f"win_w{a}", [P, T], I32, (80, 64, 82)[a])
             nc.sync.dma_start(
                 out=win_w[a][:], in_=tab[a, 0 : 512 * T].rearrange("(p b) -> p b", p=P).bitcast(I32)
             )
@@ -67,17 +67,9 @@ def tile_list_tablora_res_kernel(
         load_down(0)
         load_words(0)
 
-        w4s = keep.tile([P, PASSES, M], U8, name="w4s", align_bytes=64)
         planes = [keep.tile([P, S], U8, name=f"plane{a}", align_bytes=64) for a in range(PASSES - 1)]
-        nc.vector.memset(w4s[:].rearrange("p a n -> p (a n)").bitcast(I32), 0)
         for plane in planes:
-            nc.vector.memset(plane[:].bitcast(I32), 0)
-        w4s_rows = w4_scales.bitcast(I32)
-        for q in range(4):
-            nc.gpsimd.dma_start(
-                out=w4s[32 * q : 32 * q + 4, :, :].bitcast(I32),
-                in_=w4s_rows[:, 4 * q : 4 * q + 4, :].rearrange("a r n -> r a n"),
-            )
+            nc.gpsimd.memset(plane[:].bitcast(I32), 0)
 
         gs = keep.tile([P, S], U8, name="gs", align_bytes=64)
         nc.vector.tensor_copy(gs[:], win_s[:].bitcast(U8).indirect(offsets[:]))
@@ -143,13 +135,13 @@ def tile_list_tablora_res_kernel(
 
         quantize_down(0)
         load_down(2)
-        planes.append(staged("plane2", [P, S], U8, 0))
-        nc.vector.memset(planes[2][:].bitcast(I32), 0)
-        move_plane(2, nc.sync)
         banks = {}
         for n in (0, LAST, 1):
             gather_words(0, n)
         load_words(2)
+        planes.append(staged("plane2", [P, S], U8, 80))
+        nc.gpsimd.memset(planes[2][:].bitcast(I32), 0)
+        move_plane(2, nc.sync)
         for n in (0, LAST):
             for b in range(4):
                 banks[n, b] = open_bank()
@@ -157,12 +149,18 @@ def tile_list_tablora_res_kernel(
         quantize_down(1)
         for n in (LAST, 0, 1):
             gather_words(1, n)
-        w4w = staged("w4w", [P, PASSES, 2 * M], U8, 50)
+        w4w = staged("w4w", [P, PASSES, 2 * M], U8, 64)
         nc.sync.dma_start(
             out=w4w[:].bitcast(I32), in_=w4_words.bitcast(I32).rearrange("a p b -> p a b")
         )
-        up_raw = staged("up_raw", [P, 4, M], F32, 56)
-        nc.sync.dma_start(out=up_raw[:], in_=up.rearrange("(p j) w -> p j w", j=4))
+        w4s = staged("w4s", [P, PASSES, M], U8, 70)
+        nc.gpsimd.memset(w4s[:].rearrange("p a n -> p (a n)").bitcast(I32), 0)
+        w4s_rows = w4_scales.bitcast(I32)
+        for q in range(4):
+            nc.sync.dma_start(
+                out=w4s[32 * q : 32 * q + 4, :, :].bitcast(I32),
+                in_=w4s_rows[:, 4 * q : 4 * q + 4, :].rearrange("a r n -> r a n"),
+            )
         part = []
         for b in range(4):
             h_passes(banks[LAST, b], 1, LAST, b, False, True)
@@ -176,7 +174,9 @@ def tile_list_tablora_res_kernel(
             for a in range(2):
                 h_passes(banks[1, b], a, 1, b, a == 0, False)
         quantize_down(2)
-        res = staged("res", [P, MT, S], F32, 2)
+        up_raw = staged("up_raw", [P, 4, M], F32, 0)
+        nc.sync.dma_start(out=up_raw[:], in_=up.rearrange("(p j) w -> p j w", j=4))
+        res = staged("res", [P, MT, S], F32, 16)
         for m in range(MT):
             nc.sync.dma_start(out=res[:, m, :], in_=prev[P * m : P * (m + 1), :])
         for n in range(CHUNKS):

@@ -26,6 +26,7 @@ MT = M // P
 
 KB = 1024
 SCALE_ROWS = (16, 48, 112)
+KEPT = 6
 
 
 def tile_list_tablora_res_kernel(
@@ -69,7 +70,7 @@ def tile_list_tablora_res_kernel(
 
         planes = [keep.tile([P, S], U8, name=f"plane{a}", align_bytes=64) for a in range(PASSES - 1)]
         for plane in planes:
-            nc.gpsimd.memset(plane[:].bitcast(I32), 0)
+            nc.vector.memset(plane[:].bitcast(I32), 0)
 
         gs = keep.tile([P, S], U8, name="gs", align_bytes=64)
         nc.vector.tensor_copy(gs[:], win_s[:].bitcast(U8).indirect(offsets[:]))
@@ -90,7 +91,10 @@ def tile_list_tablora_res_kernel(
         dcodes, dscales = [], []
 
         def quantize_down(a):
-            grp = grps.tile([P, 4 * R], BF16, name="grp", align_bytes=64)
+            if a == 0:
+                grp = staged("grp0", [P, 4 * R], BF16, 98)
+            else:
+                grp = grps.tile([P, 4 * R], BF16, name="grp", align_bytes=64)
             dst = grp[:].rearrange("p (t m j) -> p m t j", t=4, j=4)
             src = raw[a][:].rearrange("p j (m t) -> p m t j", t=4)
             if a < PASSES - 1:
@@ -102,6 +106,25 @@ def tile_list_tablora_res_kernel(
             nc.vector.quantize_mx(out=c[:].bitcast(FP8X4), scales=s[:], in_=grp[:])
             dcodes.append(c)
             dscales.append(s)
+
+        w4 = {}
+
+        def load_w4(name, m0, m1, kb_words, kb_scales):
+            words = staged(name + "_words", [P, PASSES, 2 * P * (m1 - m0)], U8, kb_words)
+            scales = staged(name + "_scales", [P, PASSES, P * (m1 - m0)], U8, kb_scales)
+            nc.sync.dma_start(
+                out=words[:].bitcast(I32),
+                in_=w4_words[:, :, 2 * P * m0 : 2 * P * m1].bitcast(I32).rearrange("a p b -> p a b"),
+            )
+            nc.vector.memset(scales[:].rearrange("p a n -> p (a n)").bitcast(I32), 0)
+            scale_rows = w4_scales[:, :, P * m0 : P * m1].bitcast(I32)
+            for q in range(4):
+                nc.sync.dma_start(
+                    out=scales[32 * q : 32 * q + 4, :, :].bitcast(I32),
+                    in_=scale_rows[:, 4 * q : 4 * q + 4, :].rearrange("a r n -> r a n"),
+                )
+            for m in range(m0, m1):
+                w4[m] = (words, scales, m - m0)
 
         gw = {}
         OC = NT // 16
@@ -130,49 +153,58 @@ def tile_list_tablora_res_kernel(
                     stop=stop and t == RT - 1,
                 )
 
+        def w4_pass(bank, a, m, n):
+            words, scales, i = w4[m]
+            nc.tensor.matmul_mx(
+                out=bank[:],
+                lhsT=words[:, a, 2 * P * i : 2 * P * (i + 1)].bitcast(FP4X4),
+                lhsT_scale=scales[:, a, P * i : P * (i + 1)],
+                rhs=gw[a, n][:].bitcast(FP8X4),
+                rhs_scale=planes[a][:, NT * n : NT * (n + 1)],
+                start=(a == 0),
+                stop=False,
+            )
+
         def interleaved(bank):
             return bank[:].rearrange("p (t c) -> p c t", t=RT)
 
+        blocks = [(n, b) for n in range(CHUNKS) for b in range(4)]
+        kept, parked = blocks[:KEPT], blocks[KEPT:][::-1]
+        early = [(0, n) for n in range(8 - KEPT)]
+        first = parked + kept[: 8 - len(parked)]
+
         quantize_down(0)
         load_down(2)
+        load_w4("w4_first", 0, 1, 98, 99)
         banks = {}
-        for n in (0, LAST, 1):
+        for n in (2, 1, 0):
             gather_words(0, n)
         load_words(2)
         planes.append(staged("plane2", [P, S], U8, 80))
-        nc.gpsimd.memset(planes[2][:].bitcast(I32), 0)
+        nc.vector.memset(planes[2][:].bitcast(I32), 0)
         move_plane(2, nc.sync)
-        for n in (0, LAST):
-            for b in range(4):
+        for n, b in first:
+            banks[n, b] = open_bank()
+            h_passes(banks[n, b], 0, n, b, True, False)
+        quantize_down(1)
+        for n in (2, 1, 0):
+            gather_words(1, n)
+        load_w4("w4_rest", 1, MT, 64, 70)
+        part = {}
+        for n, b in parked:
+            h_passes(banks[n, b], 1, n, b, False, True)
+            part[n, b] = keep.tile([P, P, 4], F32, name=f"part{n}_{b}")
+            nc.scalar.copy(out=part[n, b][:], in_=interleaved(banks[n, b]))
+        for n, b in kept[::-1]:
+            if (n, b) not in first:
                 banks[n, b] = open_bank()
                 h_passes(banks[n, b], 0, n, b, True, False)
-        quantize_down(1)
-        for n in (LAST, 0, 1):
-            gather_words(1, n)
-        w4w = staged("w4w", [P, PASSES, 2 * M], U8, 64)
-        nc.sync.dma_start(
-            out=w4w[:].bitcast(I32), in_=w4_words.bitcast(I32).rearrange("a p b -> p a b")
-        )
-        w4s = staged("w4s", [P, PASSES, M], U8, 70)
-        nc.gpsimd.memset(w4s[:].rearrange("p a n -> p (a n)").bitcast(I32), 0)
-        w4s_rows = w4_scales.bitcast(I32)
-        for q in range(4):
-            nc.sync.dma_start(
-                out=w4s[32 * q : 32 * q + 4, :, :].bitcast(I32),
-                in_=w4s_rows[:, 4 * q : 4 * q + 4, :].rearrange("a r n -> r a n"),
-            )
-        part = []
-        for b in range(4):
-            h_passes(banks[LAST, b], 1, LAST, b, False, True)
-            x = keep.tile([P, P, 4], F32, name=f"part{b}")
-            nc.scalar.copy(out=x[:], in_=interleaved(banks[LAST, b]))
-            part.append(x)
-        for b in range(4):
-            h_passes(banks[0, b], 1, 0, b, False, False)
-        for b in range(4):
-            banks[1, b] = open_bank()
-            for a in range(2):
-                h_passes(banks[1, b], a, 1, b, a == 0, False)
+            h_passes(banks[n, b], 1, n, b, False, False)
+        ys = {}
+        for m, n in early:
+            ys[m, n] = open_bank()
+            for a in range(PASSES - 1):
+                w4_pass(ys[m, n], a, m, n)
         quantize_down(2)
         up_raw = staged("up_raw", [P, 4, M], F32, 0)
         nc.sync.dma_start(out=up_raw[:], in_=up.rearrange("(p j) w -> p j w", j=4))
@@ -186,13 +218,15 @@ def tile_list_tablora_res_kernel(
             grp = grps.tile([P, 4 * R], BF16, name="grp", align_bytes=64)
             for b in range(4):
                 dst = grp[:, 512 * b : 512 * (b + 1)].rearrange("p (c t) -> p c t", t=4)
-                if n < LAST:
+                if (n, b) in kept:
                     h_passes(banks[n, b], 2, n, b, False, True)
                     nc.scalar.copy(out=dst, in_=interleaved(banks[n, b]))
                 else:
                     bank = open_bank()
                     h_passes(bank, 2, n, b, True, True)
-                    nc.vector.tensor_tensor(dst, interleaved(bank), part[b][:], ADD)
+                    nc.vector.tensor_tensor(dst, interleaved(bank), part[n, b][:], ADD)
+            if (0, n) in ys:
+                w4_pass(ys[0, n], PASSES - 1, 0, n)
             c = keep.tile([P, NT], U32, name=f"hcodes{n}", align_bytes=64)
             s = keep.tile([P, NT], U8, name=f"hscales{n}", align_bytes=64)
             nc.vector.quantize_mx(out=c[:].bitcast(FP8X4), scales=s[:], in_=grp[:])
@@ -219,18 +253,11 @@ def tile_list_tablora_res_kernel(
         order += [(m, LAST) for m in range(half)]
         order += [(m, n) for m in range(half, MT) for n in range(CHUNKS)]
         for m, n in order:
-            cols = slice(NT * n, NT * (n + 1))
-            y = open_bank()
-            for a in range(PASSES):
-                nc.tensor.matmul_mx(
-                    out=y[:],
-                    lhsT=w4w[:, a, 256 * m : 256 * (m + 1)].bitcast(FP4X4),
-                    lhsT_scale=w4s[:, a, P * m : P * (m + 1)],
-                    rhs=gw[a, n][:].bitcast(FP8X4),
-                    rhs_scale=planes[a][:, cols],
-                    start=(a == 0),
-                    stop=False,
-                )
+            if (m, n) not in ys:
+                ys[m, n] = open_bank()
+                for a in range(PASSES):
+                    w4_pass(ys[m, n], a, m, n)
+            y = ys[m, n]
             nc.tensor.matmul_mx(
                 out=y[:],
                 lhsT=ucodes[:, P * m : P * (m + 1)].bitcast(FP8X4),

@@ -26,7 +26,7 @@ MT = M // P
 
 KB = 1024
 SCALE_ROWS = (16, 48, 112)
-KEPT = 6
+KEPT = 5
 
 
 def tile_list_tablora_res_kernel(
@@ -41,7 +41,7 @@ def tile_list_tablora_res_kernel(
         psum = ctx.enter_context(tc.psum_pool(name="psum", bufs=8))
 
         def staged(name, shape, dtype, kb):
-            return stage.tile(shape, dtype, name=name, offset=kb * KB, align_bytes=64)
+            return stage.tile(shape, dtype, name=name, offset=int(kb * KB), align_bytes=64)
 
         win_s = staged("win_s", [P, T // 4], I32, 62)
         rows = tab[:, 512 * T : 528 * T].rearrange("a (q t) -> a q t", q=16).bitcast(I32)
@@ -56,7 +56,7 @@ def tile_list_tablora_res_kernel(
         raw, win_w = {}, {}
 
         def load_down(a):
-            raw[a] = staged(f"raw{a}", [P, 4, R], F32, (14, 56, 14)[a])
+            raw[a] = staged(f"raw{a}", [P, 4, R], F32, (14, 24, 14)[a])
             nc.sync.dma_start(out=raw[a][:], in_=down[512 * a : 512 * (a + 1), :].rearrange("(p j) w -> p j w", j=4))
 
         def load_words(a):
@@ -66,6 +66,7 @@ def tile_list_tablora_res_kernel(
             )
 
         load_down(0)
+        load_down(1)
         load_words(0)
 
         planes = [keep.tile([P, S], U8, name=f"plane{a}", align_bytes=64) for a in range(PASSES - 1)]
@@ -84,9 +85,8 @@ def tile_list_tablora_res_kernel(
                 )
 
         move_plane(0, nc.sync)
-        load_down(1)
-        move_plane(1, nc.sync)
         load_words(1)
+        move_plane(1, nc.sync)
 
         dcodes, dscales = [], []
 
@@ -193,7 +193,10 @@ def tile_list_tablora_res_kernel(
         part = {}
         for n, b in parked:
             h_passes(banks[n, b], 1, n, b, False, True)
-            part[n, b] = keep.tile([P, P, 4], F32, name=f"part{n}_{b}")
+            if n == LAST and b < 2:
+                part[n, b] = staged(f"part{n}_{b}", [P, P, 4], F32, 104 + 2 * b)
+            else:
+                part[n, b] = keep.tile([P, P, 4], F32, name=f"part{n}_{b}")
             nc.scalar.copy(out=part[n, b][:], in_=interleaved(banks[n, b]))
         for n, b in kept[::-1]:
             if (n, b) not in first:
@@ -213,11 +216,54 @@ def tile_list_tablora_res_kernel(
             nc.sync.dma_start(out=res[:, m, :], in_=prev[P * m : P * (m + 1), :])
         for n in range(CHUNKS):
             gather_words(2, n)
-        hcodes, hscales = [], []
+        ucodes = keep.tile([P, M], U32, name="ucodes", align_bytes=64)
+        uscales = keep.tile([P, M], U8, name="uscales", align_bytes=64)
+
+        def quantize_up(i):
+            cols = slice(256 * i, 256 * (i + 1))
+            if i == 0:
+                up_grp = staged("up_grp0", [P, 256, 4], BF16, 102)
+            else:
+                up_grp = keep.tile([P, 256, 4], BF16, name=f"up_grp{i}", align_bytes=64)
+            nc.scalar.copy(
+                out=up_grp[:].rearrange("p (c i) j -> p c j i", i=4),
+                in_=up_raw[:, :, cols].rearrange("p j (c i) -> p c j i", i=4),
+            )
+            nc.vector.quantize_mx(
+                out=ucodes[:, cols].bitcast(FP8X4),
+                scales=uscales[:, cols],
+                in_=up_grp[:].rearrange("p c j -> p (c j)"),
+            )
+
+        hcodes, hscales, h_pieces = {}, {}, {}
+
+        def quantize_h(n):
+            if n < LAST:
+                hcodes[n] = staged(f"hcodes{n}", [P, NT], U32, 104.5 + 2 * n)
+            else:
+                hcodes[n] = keep.tile([P, NT], U32, name=f"hcodes{n}", align_bytes=64)
+            hscales[n] = keep.tile([P, NT], U8, name=f"hscales{n}", align_bytes=64)
+            for tile, b0, b1 in h_pieces[n]:
+                cols = slice(P * b0, P * b1)
+                nc.vector.quantize_mx(
+                    out=hcodes[n][:, cols].bitcast(FP8X4),
+                    scales=hscales[n][:, cols],
+                    in_=tile[:, 0 : 512 * (b1 - b0)],
+                )
+
         for n in range(CHUNKS):
             grp = grps.tile([P, 4 * R], BF16, name="grp", align_bytes=64)
+            pieces = [(grp, 0, 4)]
+            if n == LAST:
+                pieces = [(grp, 0, 2), (staged("grp_tail", [P, 2 * R], BF16, 102), 2, 4)]
+            h_pieces[n] = pieces
             for b in range(4):
-                dst = grp[:, 512 * b : 512 * (b + 1)].rearrange("p (c t) -> p c t", t=4)
+                if (n, b) == (LAST, 2):
+                    quantize_h(0)
+                    quantize_h(1)
+                    quantize_up(0)
+                tile, b0, b1 = [piece for piece in pieces if piece[1] <= b < piece[2]][0]
+                dst = tile[:, 512 * (b - b0) : 512 * (b - b0 + 1)].rearrange("p (c t) -> p c t", t=4)
                 if (n, b) in kept:
                     h_passes(banks[n, b], 2, n, b, False, True)
                     nc.scalar.copy(out=dst, in_=interleaved(banks[n, b]))
@@ -227,32 +273,17 @@ def tile_list_tablora_res_kernel(
                     nc.vector.tensor_tensor(dst, interleaved(bank), part[n, b][:], ADD)
             if (0, n) in ys:
                 w4_pass(ys[0, n], PASSES - 1, 0, n)
-            c = keep.tile([P, NT], U32, name=f"hcodes{n}", align_bytes=64)
-            s = keep.tile([P, NT], U8, name=f"hscales{n}", align_bytes=64)
-            nc.vector.quantize_mx(out=c[:].bitcast(FP8X4), scales=s[:], in_=grp[:])
-            hcodes.append(c)
-            hscales.append(s)
+        quantize_h(LAST)
 
-        up_grp = keep.tile([P, M, 4], BF16, name="up_grp", align_bytes=64)
-        ucodes = keep.tile([P, M], U32, name="ucodes", align_bytes=64)
-        uscales = keep.tile([P, M], U8, name="uscales", align_bytes=64)
-        for i in range(4):
-            cols = slice(256 * i, 256 * (i + 1))
-            nc.scalar.copy(
-                out=up_grp[:, cols, :].rearrange("p (c i) j -> p c j i", i=4),
-                in_=up_raw[:, :, cols].rearrange("p j (c i) -> p c j i", i=4),
-            )
-            nc.vector.quantize_mx(
-                out=ucodes[:, cols].bitcast(FP8X4),
-                scales=uscales[:, cols],
-                in_=up_grp[:, cols, :].rearrange("p c j -> p (c j)"),
-            )
+        quantize_up(1)
 
         half = 2
         order = [(m, n) for m in range(half) for n in range(LAST)]
         order += [(m, LAST) for m in range(half)]
         order += [(m, n) for m in range(half, MT) for n in range(CHUNKS)]
         for m, n in order:
+            if m in (2, 4) and n == 0:
+                quantize_up(m // 2 + 1)
             if (m, n) not in ys:
                 ys[m, n] = open_bank()
                 for a in range(PASSES):

@@ -38,6 +38,7 @@ def tile_list_tablora_res_kernel(
         keep = ctx.enter_context(tc.tile_pool(name="keep", bufs=1))
         stage = ctx.enter_context(tc.tile_pool(name="stage", bufs=1))
         grps = ctx.enter_context(tc.tile_pool(name="grps", bufs=3))
+        ups = ctx.enter_context(tc.tile_pool(name="ups", bufs=2))
         psum = ctx.enter_context(tc.psum_pool(name="psum", bufs=8))
 
         def staged(name, shape, dtype, kb):
@@ -193,8 +194,8 @@ def tile_list_tablora_res_kernel(
         part = {}
         for n, b in parked:
             h_passes(banks[n, b], 1, n, b, False, True)
-            if n == LAST and b < 2:
-                part[n, b] = staged(f"part{n}_{b}", [P, P, 4], F32, 104 + 2 * b)
+            if n == LAST and b >= 2:
+                part[n, b] = staged(f"part{n}_{b}", [P, P, 4], F32, 100 + 2 * b)
             else:
                 part[n, b] = keep.tile([P, P, 4], F32, name=f"part{n}_{b}")
             nc.scalar.copy(out=part[n, b][:], in_=interleaved(banks[n, b]))
@@ -216,54 +217,28 @@ def tile_list_tablora_res_kernel(
             nc.sync.dma_start(out=res[:, m, :], in_=prev[P * m : P * (m + 1), :])
         for n in range(CHUNKS):
             gather_words(2, n)
-        ucodes = keep.tile([P, M], U32, name="ucodes", align_bytes=64)
-        uscales = keep.tile([P, M], U8, name="uscales", align_bytes=64)
+        ucodes, uscales = {}, {}
 
         def quantize_up(i):
             cols = slice(256 * i, 256 * (i + 1))
-            if i == 0:
-                up_grp = staged("up_grp0", [P, 256, 4], BF16, 102)
-            else:
-                up_grp = keep.tile([P, 256, 4], BF16, name=f"up_grp{i}", align_bytes=64)
+            up_grp = keep.tile([P, 256, 4], BF16, name=f"up_grp{i}", align_bytes=64)
             nc.scalar.copy(
                 out=up_grp[:].rearrange("p (c i) j -> p c j i", i=4),
                 in_=up_raw[:, :, cols].rearrange("p j (c i) -> p c j i", i=4),
             )
+            ucodes[i] = ups.tile([P, 256], U32, name="ucodes", align_bytes=64)
+            uscales[i] = ups.tile([P, 256], U8, name="uscales", align_bytes=64)
             nc.vector.quantize_mx(
-                out=ucodes[:, cols].bitcast(FP8X4),
-                scales=uscales[:, cols],
+                out=ucodes[i][:].bitcast(FP8X4),
+                scales=uscales[i][:],
                 in_=up_grp[:].rearrange("p c j -> p (c j)"),
             )
 
-        hcodes, hscales, h_pieces = {}, {}, {}
-
-        def quantize_h(n):
-            if n < LAST:
-                hcodes[n] = staged(f"hcodes{n}", [P, NT], U32, 104.5 + 2 * n)
-            else:
-                hcodes[n] = keep.tile([P, NT], U32, name=f"hcodes{n}", align_bytes=64)
-            hscales[n] = keep.tile([P, NT], U8, name=f"hscales{n}", align_bytes=64)
-            for tile, b0, b1 in h_pieces[n]:
-                cols = slice(P * b0, P * b1)
-                nc.vector.quantize_mx(
-                    out=hcodes[n][:, cols].bitcast(FP8X4),
-                    scales=hscales[n][:, cols],
-                    in_=tile[:, 0 : 512 * (b1 - b0)],
-                )
-
+        h_grp = {}
         for n in range(CHUNKS):
-            grp = grps.tile([P, 4 * R], BF16, name="grp", align_bytes=64)
-            pieces = [(grp, 0, 4)]
-            if n == LAST:
-                pieces = [(grp, 0, 2), (staged("grp_tail", [P, 2 * R], BF16, 102), 2, 4)]
-            h_pieces[n] = pieces
+            h_grp[n] = grps.tile([P, 4 * R], BF16, name="grp", align_bytes=64)
             for b in range(4):
-                if (n, b) == (LAST, 2):
-                    quantize_h(0)
-                    quantize_h(1)
-                    quantize_up(0)
-                tile, b0, b1 = [piece for piece in pieces if piece[1] <= b < piece[2]][0]
-                dst = tile[:, 512 * (b - b0) : 512 * (b - b0 + 1)].rearrange("p (c t) -> p c t", t=4)
+                dst = h_grp[n][:, 512 * b : 512 * (b + 1)].rearrange("p (c t) -> p c t", t=4)
                 if (n, b) in kept:
                     h_passes(banks[n, b], 2, n, b, False, True)
                     nc.scalar.copy(out=dst, in_=interleaved(banks[n, b]))
@@ -273,8 +248,15 @@ def tile_list_tablora_res_kernel(
                     nc.vector.tensor_tensor(dst, interleaved(bank), part[n, b][:], ADD)
             if (0, n) in ys:
                 w4_pass(ys[0, n], PASSES - 1, 0, n)
-        quantize_h(LAST)
-
+        hcodes, hscales = {}, {}
+        for n in range(CHUNKS):
+            if n < LAST:
+                hcodes[n] = staged(f"hcodes{n}", [P, NT], U32, 104.5 + 2 * n)
+            else:
+                hcodes[n] = keep.tile([P, NT], U32, name=f"hcodes{n}", align_bytes=64)
+            hscales[n] = keep.tile([P, NT], U8, name=f"hscales{n}", align_bytes=64)
+            nc.vector.quantize_mx(out=hcodes[n][:].bitcast(FP8X4), scales=hscales[n][:], in_=h_grp[n][:])
+        quantize_up(0)
         quantize_up(1)
 
         half = 2
@@ -284,6 +266,7 @@ def tile_list_tablora_res_kernel(
         for m, n in order:
             if m in (2, 4) and n == 0:
                 quantize_up(m // 2 + 1)
+            ucols = slice(P * (m % 2), P * (m % 2 + 1))
             if (m, n) not in ys:
                 ys[m, n] = open_bank()
                 for a in range(PASSES):
@@ -291,8 +274,8 @@ def tile_list_tablora_res_kernel(
             y = ys[m, n]
             nc.tensor.matmul_mx(
                 out=y[:],
-                lhsT=ucodes[:, P * m : P * (m + 1)].bitcast(FP8X4),
-                lhsT_scale=uscales[:, P * m : P * (m + 1)],
+                lhsT=ucodes[m // 2][:, ucols].bitcast(FP8X4),
+                lhsT_scale=uscales[m // 2][:, ucols],
                 rhs=hcodes[n][:].bitcast(FP8X4),
                 rhs_scale=hscales[n][:],
                 start=False,

@@ -38,7 +38,6 @@ def tile_list_tablora_res_kernel(
         keep = ctx.enter_context(tc.tile_pool(name="keep", bufs=1))
         stage = ctx.enter_context(tc.tile_pool(name="stage", bufs=1))
         grps = ctx.enter_context(tc.tile_pool(name="grps", bufs=3))
-        ups = ctx.enter_context(tc.tile_pool(name="ups", bufs=2))
         psum = ctx.enter_context(tc.psum_pool(name="psum", bufs=8))
 
         def staged(name, shape, dtype, kb):
@@ -178,7 +177,7 @@ def tile_list_tablora_res_kernel(
         load_down(2)
         load_w4("w4_first", 0, 1, 98, 99)
         banks = {}
-        for n in (2, 1, 0):
+        for n in (1, 2, 0):
             gather_words(0, n)
         load_words(2)
         planes.append(staged("plane2", [P, S], U8, 80))
@@ -221,13 +220,16 @@ def tile_list_tablora_res_kernel(
 
         def quantize_up(i):
             cols = slice(256 * i, 256 * (i + 1))
-            up_grp = keep.tile([P, 256, 4], BF16, name=f"up_grp{i}", align_bytes=64)
+            if i == 0:
+                up_grp = staged("up_grp0", [P, 256, 4], BF16, 109)
+            else:
+                up_grp = keep.tile([P, 256, 4], BF16, name=f"up_grp{i}", align_bytes=64)
             nc.scalar.copy(
                 out=up_grp[:].rearrange("p (c i) j -> p c j i", i=4),
                 in_=up_raw[:, :, cols].rearrange("p j (c i) -> p c j i", i=4),
             )
-            ucodes[i] = ups.tile([P, 256], U32, name="ucodes", align_bytes=64)
-            uscales[i] = ups.tile([P, 256], U8, name="uscales", align_bytes=64)
+            ucodes[i] = staged(f"ucodes{i}", [P, 256], U32, (112, 113, 114, 113)[i])
+            uscales[i] = keep.tile([P, 256], U8, name=f"uscales{i}", align_bytes=64)
             nc.vector.quantize_mx(
                 out=ucodes[i][:].bitcast(FP8X4),
                 scales=uscales[i][:],
@@ -250,21 +252,18 @@ def tile_list_tablora_res_kernel(
                 w4_pass(ys[0, n], PASSES - 1, 0, n)
         hcodes, hscales = {}, {}
         for n in range(CHUNKS):
-            if n < LAST:
-                hcodes[n] = staged(f"hcodes{n}", [P, NT], U32, 104.5 + 2 * n)
-            else:
-                hcodes[n] = keep.tile([P, NT], U32, name=f"hcodes{n}", align_bytes=64)
+            if n == 1:
+                quantize_up(0)
+            hcodes[n] = staged(f"hcodes{n}", [P, NT], U32, (105, 107.5, 109.5)[n])
             hscales[n] = keep.tile([P, NT], U8, name=f"hscales{n}", align_bytes=64)
             nc.vector.quantize_mx(out=hcodes[n][:].bitcast(FP8X4), scales=hscales[n][:], in_=h_grp[n][:])
-        quantize_up(0)
         quantize_up(1)
 
         half = 2
-        order = [(m, n) for m in range(half) for n in range(LAST)]
-        order += [(m, LAST) for m in range(half)]
+        order = [(m, n) for n in range(CHUNKS) for m in range(half)]
         order += [(m, n) for m in range(half, MT) for n in range(CHUNKS)]
         for m, n in order:
-            if m in (2, 4) and n == 0:
+            if (m, n) in ((2, 0), (4, 0)):
                 quantize_up(m // 2 + 1)
             ucols = slice(P * (m % 2), P * (m % 2 + 1))
             if (m, n) not in ys:

@@ -41,7 +41,7 @@ def tile_list_tablora_res_kernel(
         psum = ctx.enter_context(tc.psum_pool(name="psum", bufs=8))
 
         def staged(name, shape, dtype, kb):
-            return stage.tile(shape, dtype, name=name, offset=int(kb * KB), align_bytes=64)
+            return stage.tile(shape, dtype, name=name, offset=int(kb * KB), align_bytes=256)
 
         win_s = staged("win_s", [P, T // 4], I32, 62)
         rows = tab[:, 512 * T : 528 * T].rearrange("a (q t) -> a q t", q=16).bitcast(I32)

@@ -27,6 +27,7 @@ MT = M // P
 KB = 1024
 SCALE_ROWS = (16, 48, 112)
 KEPT = 5
+MOVING_CODES, MOVING_SCALES = 192, 64
 
 
 def tile_list_tablora_res_kernel(
@@ -40,8 +41,10 @@ def tile_list_tablora_res_kernel(
         grps = ctx.enter_context(tc.tile_pool(name="grps", bufs=3))
         psum = ctx.enter_context(tc.psum_pool(name="psum", bufs=8))
 
-        def staged(name, shape, dtype, kb):
-            return stage.tile(shape, dtype, name=name, offset=int(kb * KB), align_bytes=256)
+        def staged(name, shape, dtype, kb, phase=0):
+            return stage.tile(
+                shape, dtype, name=name, offset=int(kb * KB) + phase, align_bytes=64 if phase else 256
+            )
 
         win_s = staged("win_s", [P, T // 4], I32, 62)
         rows = tab[:, 512 * T : 528 * T].rearrange("a (q t) -> a q t", q=16).bitcast(I32)
@@ -69,7 +72,7 @@ def tile_list_tablora_res_kernel(
         load_down(1)
         load_words(0)
 
-        planes = [keep.tile([P, S], U8, name=f"plane{a}", align_bytes=64) for a in range(PASSES - 1)]
+        planes = [staged(f"plane{a}", [P, S], U8, 135 + 1.5 * a, MOVING_SCALES) for a in range(PASSES - 1)]
         for plane in planes:
             nc.vector.memset(plane[:].bitcast(I32), 0)
 
@@ -101,8 +104,8 @@ def tile_list_tablora_res_kernel(
                 nc.scalar.copy(out=dst, in_=src)
             else:
                 nc.vector.tensor_copy(out=dst, in_=src)
-            c = keep.tile([P, R], U32, name=f"dcodes{a}", align_bytes=64)
-            s = keep.tile([P, R], U8, name=f"dscales{a}", align_bytes=64)
+            c = staged(f"dcodes{a}", [P, R], U32, 142 + 2 * a)
+            s = staged(f"dscales{a}", [P, R], U8, 148 + 0.5 * a)
             nc.vector.quantize_mx(out=c[:].bitcast(FP8X4), scales=s[:], in_=grp[:])
             dcodes.append(c)
             dscales.append(s)
@@ -130,7 +133,7 @@ def tile_list_tablora_res_kernel(
         OC = NT // 16
 
         def gather_words(a, n):
-            t = keep.tile([P, NT], U32, name=f"gw{a}_{n}", align_bytes=64)
+            t = staged(f"gw{a}_{n}", [P, NT], U32, 116 + 2 * (CHUNKS * a + n), MOVING_CODES)
             nc.vector.tensor_copy(
                 t[:], win_w[a][:].bitcast(U32).indirect(offsets[:, OC * n : OC * (n + 1)])
             )
@@ -180,7 +183,7 @@ def tile_list_tablora_res_kernel(
         for n in (1, 2, 0):
             gather_words(0, n)
         load_words(2)
-        planes.append(staged("plane2", [P, S], U8, 80))
+        planes.append(staged("plane2", [P, S], U8, 80, MOVING_SCALES))
         nc.vector.memset(planes[2][:].bitcast(I32), 0)
         move_plane(2, nc.sync)
         for n, b in first:
@@ -229,7 +232,7 @@ def tile_list_tablora_res_kernel(
                 in_=up_raw[:, :, cols].rearrange("p j (c i) -> p c j i", i=4),
             )
             ucodes[i] = staged(f"ucodes{i}", [P, 256], U32, (112, 113, 114, 113)[i])
-            uscales[i] = keep.tile([P, 256], U8, name=f"uscales{i}", align_bytes=64)
+            uscales[i] = staged(f"uscales{i}", [P, 256], U8, 141 + 0.25 * i)
             nc.vector.quantize_mx(
                 out=ucodes[i][:].bitcast(FP8X4),
                 scales=uscales[i][:],
@@ -254,8 +257,8 @@ def tile_list_tablora_res_kernel(
         for n in range(CHUNKS):
             if n == 1:
                 quantize_up(0)
-            hcodes[n] = staged(f"hcodes{n}", [P, NT], U32, (105, 107.5, 109.5)[n])
-            hscales[n] = keep.tile([P, NT], U8, name=f"hscales{n}", align_bytes=64)
+            hcodes[n] = staged(f"hcodes{n}", [P, NT], U32, (105, 107.5, 109.5)[n], MOVING_CODES)
+            hscales[n] = staged(f"hscales{n}", [P, NT], U8, 139 + 0.5 * n, MOVING_SCALES)
             nc.vector.quantize_mx(out=hcodes[n][:].bitcast(FP8X4), scales=hscales[n][:], in_=h_grp[n][:])
         quantize_up(1)
 

@@ -25,7 +25,7 @@ MT = M // P
 
 
 KB = 1024
-SCALE_ROWS = (16, 48, 112)
+FIRST_SCALE_ROW = 48
 KEPT = 5
 MOVING_CODES, MOVING_SCALES = 192, 64
 
@@ -46,13 +46,19 @@ def tile_list_tablora_res_kernel(
                 shape, dtype, name=name, offset=int(kb * KB) + phase, align_bytes=64 if phase else 256
             )
 
+        def zeroed_w4_scales(name, tiles, kb):
+            scales = staged(name, [P, PASSES, P * tiles], U8, kb)
+            nc.vector.memset(scales[:].rearrange("p a n -> p (a n)").bitcast(I32), 0)
+            return scales
+
+        first_scales = zeroed_w4_scales("w4_first_scales", 1, 153)
+
         win_s = staged("win_s", [P, T // 4], I32, 62)
         rows = tab[:, 512 * T : 528 * T].rearrange("a (q t) -> a q t", q=16).bitcast(I32)
-        for a in (0, 2, 1):
-            nc.sync.dma_start(out=win_s[SCALE_ROWS[a] : SCALE_ROWS[a] + 16, :], in_=rows[a])
-        nc.vector.memset(win_s[0:16, :], 0)
-        nc.gpsimd.memset(win_s[32:48, :], 0)
-        nc.gpsimd.memset(win_s[64:112, :], 0)
+        for a in range(PASSES):
+            nc.sync.dma_start(out=win_s[FIRST_SCALE_ROW + a : FIRST_SCALE_ROW + 48 : PASSES, :], in_=rows[a])
+        nc.vector.memset(win_s[0:FIRST_SCALE_ROW, :], 0)
+        nc.vector.memset(win_s[FIRST_SCALE_ROW + 48 : P, :], 0)
         offsets = lists.tile([P, S // 16], U16, name="offsets")
         nc.sync.dma_start(offsets[:], offs)
 
@@ -68,28 +74,47 @@ def tile_list_tablora_res_kernel(
                 out=win_w[a][:], in_=tab[a, 0 : 512 * T].rearrange("(p b) -> p b", p=P).bitcast(I32)
             )
 
+        w4 = {}
+
+        def load_w4(name, m0, m1, kb_words, scales):
+            words = staged(name + "_words", [P, PASSES, 2 * P * (m1 - m0)], U8, kb_words)
+            nc.sync.dma_start(
+                out=words[:].bitcast(I32),
+                in_=w4_words[:, :, 2 * P * m0 : 2 * P * m1].bitcast(I32).rearrange("a p b -> p a b"),
+            )
+            scale_rows = w4_scales[:, :, P * m0 : P * m1].bitcast(I32)
+            for q in range(4):
+                nc.sync.dma_start(
+                    out=scales[32 * q : 32 * q + 4, :, :].bitcast(I32),
+                    in_=scale_rows[:, 4 * q : 4 * q + 4, :].rearrange("a r n -> r a n"),
+                )
+            for m in range(m0, m1):
+                w4[m] = (words, scales, m - m0)
+
         load_down(0)
+        load_w4("w4_first", 0, 1, 152, first_scales)
         load_down(1)
         load_words(0)
 
-        planes = [staged(f"plane{a}", [P, S], U8, 135 + 1.5 * a, MOVING_SCALES) for a in range(PASSES - 1)]
+        planes = [staged(f"plane{a}", [P, S], U8, 154 + 1.5 * a, MOVING_SCALES) for a in range(PASSES)]
         for plane in planes:
             nc.vector.memset(plane[:].bitcast(I32), 0)
 
         gs = keep.tile([P, S], U8, name="gs", align_bytes=64)
         nc.vector.tensor_copy(gs[:], win_s[:].bitcast(U8).indirect(offsets[:]))
 
-        def move_plane(a, queue):
-            for q in range(4):
-                first = SCALE_ROWS[a] + 4 * q
+        def move_plane(a, queue, quadrants=range(4)):
+            for q in quadrants:
+                first = FIRST_SCALE_ROW + 4 * PASSES * q
                 queue.dma_start(
                     out=planes[a][32 * q : 32 * q + 4, :].bitcast(I32),
-                    in_=gs[first : first + 4, :].bitcast(I32),
+                    in_=gs[first + a : first + 4 * PASSES : PASSES, :].bitcast(I32),
                 )
 
         move_plane(0, nc.sync)
+        move_plane(1, nc.sync, range(2))
         load_words(1)
-        move_plane(1, nc.sync)
+        move_plane(1, nc.sync, range(2, 4))
 
         dcodes, dscales = [], []
 
@@ -109,25 +134,6 @@ def tile_list_tablora_res_kernel(
             nc.vector.quantize_mx(out=c[:].bitcast(FP8X4), scales=s[:], in_=grp[:])
             dcodes.append(c)
             dscales.append(s)
-
-        w4 = {}
-
-        def load_w4(name, m0, m1, kb_words, kb_scales):
-            words = staged(name + "_words", [P, PASSES, 2 * P * (m1 - m0)], U8, kb_words)
-            scales = staged(name + "_scales", [P, PASSES, P * (m1 - m0)], U8, kb_scales)
-            nc.sync.dma_start(
-                out=words[:].bitcast(I32),
-                in_=w4_words[:, :, 2 * P * m0 : 2 * P * m1].bitcast(I32).rearrange("a p b -> p a b"),
-            )
-            nc.vector.memset(scales[:].rearrange("p a n -> p (a n)").bitcast(I32), 0)
-            scale_rows = w4_scales[:, :, P * m0 : P * m1].bitcast(I32)
-            for q in range(4):
-                nc.sync.dma_start(
-                    out=scales[32 * q : 32 * q + 4, :, :].bitcast(I32),
-                    in_=scale_rows[:, 4 * q : 4 * q + 4, :].rearrange("a r n -> r a n"),
-                )
-            for m in range(m0, m1):
-                w4[m] = (words, scales, m - m0)
 
         gw = {}
         OC = NT // 16
@@ -178,21 +184,19 @@ def tile_list_tablora_res_kernel(
 
         quantize_down(0)
         load_down(2)
-        load_w4("w4_first", 0, 1, 98, 99)
+        move_plane(2, nc.sync, range(3))
         banks = {}
         for n in (1, 2, 0):
             gather_words(0, n)
         load_words(2)
-        planes.append(staged("plane2", [P, S], U8, 80, MOVING_SCALES))
-        nc.vector.memset(planes[2][:].bitcast(I32), 0)
-        move_plane(2, nc.sync)
+        move_plane(2, nc.sync, range(3, 4))
         for n, b in first:
             banks[n, b] = open_bank()
             h_passes(banks[n, b], 0, n, b, True, False)
         quantize_down(1)
         for n in (2, 1, 0):
             gather_words(1, n)
-        load_w4("w4_rest", 1, MT, 64, 70)
+        load_w4("w4_rest", 1, MT, 64, zeroed_w4_scales("w4_rest_scales", MT - 1, 70))
         part = {}
         for n, b in parked:
             h_passes(banks[n, b], 1, n, b, False, True)

@@ -51,7 +51,7 @@ def tile_list_tablora_res_kernel(
             nc.vector.memset(scales[:].rearrange("p a n -> p (a n)").bitcast(I32), 0)
             return scales
 
-        first_scales = zeroed_w4_scales("w4_first_scales", 1, 153)
+        first_scales = zeroed_w4_scales("w4_first_scales", 1, 160)
 
         win_s = staged("win_s", [P, T // 4], I32, 62)
         rows = tab[:, 512 * T : 528 * T].rearrange("a (q t) -> a q t", q=16).bitcast(I32)
@@ -74,14 +74,18 @@ def tile_list_tablora_res_kernel(
                 out=win_w[a][:], in_=tab[a, 0 : 512 * T].rearrange("(p b) -> p b", p=P).bitcast(I32)
             )
 
-        w4 = {}
+        w4_codes, w4_planes = {}, {}
 
-        def load_w4(name, m0, m1, kb_words, scales):
-            words = staged(name + "_words", [P, PASSES, 2 * P * (m1 - m0)], U8, kb_words)
+        def load_w4_words(name, m0, m1, kb):
+            words = staged(name, [P, PASSES, 2 * P * (m1 - m0)], U8, kb)
             nc.sync.dma_start(
                 out=words[:].bitcast(I32),
                 in_=w4_words[:, :, 2 * P * m0 : 2 * P * m1].bitcast(I32).rearrange("a p b -> p a b"),
             )
+            for m in range(m0, m1):
+                w4_codes[m] = (words, m - m0)
+
+        def load_w4_scales(scales, m0, m1):
             scale_rows = w4_scales[:, :, P * m0 : P * m1].bitcast(I32)
             for q in range(4):
                 nc.sync.dma_start(
@@ -89,10 +93,9 @@ def tile_list_tablora_res_kernel(
                     in_=scale_rows[:, 4 * q : 4 * q + 4, :].rearrange("a r n -> r a n"),
                 )
             for m in range(m0, m1):
-                w4[m] = (words, scales, m - m0)
+                w4_planes[m] = (scales, m - m0)
 
         load_down(0)
-        load_w4("w4_first", 0, 1, 152, first_scales)
         load_down(1)
         load_words(0)
 
@@ -103,8 +106,8 @@ def tile_list_tablora_res_kernel(
         gs = keep.tile([P, S], U8, name="gs", align_bytes=64)
         nc.vector.tensor_copy(gs[:], win_s[:].bitcast(U8).indirect(offsets[:]))
 
-        def move_plane(a, queue, quadrants=range(4)):
-            for q in quadrants:
+        def move_plane(a, queue):
+            for q in range(4):
                 first = FIRST_SCALE_ROW + 4 * PASSES * q
                 queue.dma_start(
                     out=planes[a][32 * q : 32 * q + 4, :].bitcast(I32),
@@ -112,9 +115,8 @@ def tile_list_tablora_res_kernel(
                 )
 
         move_plane(0, nc.sync)
-        move_plane(1, nc.sync, range(2))
         load_words(1)
-        move_plane(1, nc.sync, range(2, 4))
+        move_plane(1, nc.sync)
 
         dcodes, dscales = [], []
 
@@ -162,15 +164,15 @@ def tile_list_tablora_res_kernel(
                     stop=stop and t == RT - 1,
                 )
 
-        def w4_pass(bank, a, m, n):
-            words, scales, i = w4[m]
+        def w4_pass(bank, a, m, n, c0=0, c1=NT, start=True):
+            (words, i), (scales, j) = w4_codes[m], w4_planes[m]
             nc.tensor.matmul_mx(
-                out=bank[:],
+                out=bank,
                 lhsT=words[:, a, 2 * P * i : 2 * P * (i + 1)].bitcast(FP4X4),
-                lhsT_scale=scales[:, a, P * i : P * (i + 1)],
-                rhs=gw[a, n][:].bitcast(FP8X4),
-                rhs_scale=planes[a][:, NT * n : NT * (n + 1)],
-                start=(a == 0),
+                lhsT_scale=scales[:, a, P * j : P * (j + 1)],
+                rhs=gw[a, n][:, c0:c1].bitcast(FP8X4),
+                rhs_scale=planes[a][:, NT * n + c0 : NT * n + c1],
+                start=(a == 0 and start),
                 stop=False,
             )
 
@@ -179,24 +181,26 @@ def tile_list_tablora_res_kernel(
 
         blocks = [(n, b) for n in range(CHUNKS) for b in range(4)]
         kept, parked = blocks[:KEPT], blocks[KEPT:][::-1]
-        early = [(0, n) for n in range(8 - KEPT)]
+        early = [(i // CHUNKS, i % CHUNKS) for i in range(8 - KEPT)]
         first = parked + kept[: 8 - len(parked)]
 
         quantize_down(0)
         load_down(2)
-        move_plane(2, nc.sync, range(3))
+        load_w4_words("w4_first_words", 0, 1, 152)
+        load_w4_scales(first_scales, 0, 1)
         banks = {}
         for n in (1, 2, 0):
             gather_words(0, n)
         load_words(2)
-        move_plane(2, nc.sync, range(3, 4))
+        move_plane(2, nc.sync)
         for n, b in first:
             banks[n, b] = open_bank()
             h_passes(banks[n, b], 0, n, b, True, False)
         quantize_down(1)
         for n in (2, 1, 0):
             gather_words(1, n)
-        load_w4("w4_rest", 1, MT, 64, zeroed_w4_scales("w4_rest_scales", MT - 1, 70))
+        load_w4_words("w4_rest_words", 1, MT, 64)
+        rest_scales = zeroed_w4_scales("w4_rest_scales", MT - 1, 70)
         part = {}
         for n, b in parked:
             h_passes(banks[n, b], 1, n, b, False, True)
@@ -214,10 +218,13 @@ def tile_list_tablora_res_kernel(
         for m, n in early:
             ys[m, n] = open_bank()
             for a in range(PASSES - 1):
-                w4_pass(ys[m, n], a, m, n)
+                w4_pass(ys[m, n][:], a, m, n)
         quantize_down(2)
         up_raw = staged("up_raw", [P, 4, M], F32, 0)
-        nc.sync.dma_start(out=up_raw[:], in_=up.rearrange("(p j) w -> p j w", j=4))
+        up_rows = up.rearrange("(p j) w -> p j w", j=4)
+        nc.sync.dma_start(out=up_raw[:, 0:2, :], in_=up_rows[:, 0:2, :])
+        load_w4_scales(rest_scales, 1, MT)
+        nc.sync.dma_start(out=up_raw[:, 2:4, :], in_=up_rows[:, 2:4, :])
         res = staged("res", [P, MT, S], F32, 16)
         for m in range(MT):
             nc.sync.dma_start(out=res[:, m, :], in_=prev[P * m : P * (m + 1), :])
@@ -255,8 +262,9 @@ def tile_list_tablora_res_kernel(
                     bank = open_bank()
                     h_passes(bank, 2, n, b, True, True)
                     nc.vector.tensor_tensor(dst, interleaved(bank), part[n, b][:], ADD)
-            if (0, n) in ys:
-                w4_pass(ys[0, n], PASSES - 1, 0, n)
+            for m in range(2):
+                if (m, n) in ys:
+                    w4_pass(ys[m, n][:], PASSES - 1, m, n)
         hcodes, hscales = {}, {}
         for n in range(CHUNKS):
             if n == 1:
@@ -269,30 +277,48 @@ def tile_list_tablora_res_kernel(
         half = 2
         order = [(m, n) for n in range(CHUNKS) for m in range(half)]
         order += [(m, n) for m in range(half, MT) for n in range(CHUNKS)]
-        for m, n in order:
+
+        def up_pass(bank, m, n, c0=0, c1=NT, stop=True):
+            ucols = slice(P * (m % 2), P * (m % 2 + 1))
+            nc.tensor.matmul_mx(
+                out=bank,
+                lhsT=ucodes[m // 2][:, ucols].bitcast(FP8X4),
+                lhsT_scale=uscales[m // 2][:, ucols],
+                rhs=hcodes[n][:, c0:c1].bitcast(FP8X4),
+                rhs_scale=hscales[n][:, c0:c1],
+                start=False,
+                stop=stop,
+            )
+
+        def add_prev(bank, m, first, width):
+            cols = slice(first, first + width)
+            nc.vector.tensor_tensor(res[:, m, cols], bank, res[:, m, cols], ADD)
+
+        def store(m, first, width):
+            cols = slice(first, first + width)
+            nc.scalar.dma_start(out=out[P * m : P * (m + 1), cols], in_=res[:, m, cols])
+
+        for m, n in order[:-1]:
             if (m, n) in ((2, 0), (4, 0)):
                 quantize_up(m // 2 + 1)
-            ucols = slice(P * (m % 2), P * (m % 2 + 1))
             if (m, n) not in ys:
                 ys[m, n] = open_bank()
                 for a in range(PASSES):
-                    w4_pass(ys[m, n], a, m, n)
-            y = ys[m, n]
-            nc.tensor.matmul_mx(
-                out=y[:],
-                lhsT=ucodes[m // 2][:, ucols].bitcast(FP8X4),
-                lhsT_scale=uscales[m // 2][:, ucols],
-                rhs=hcodes[n][:].bitcast(FP8X4),
-                rhs_scale=hscales[n][:],
-                start=False,
-                stop=True,
-            )
-            halves = 2 if m == MT - 1 and n == LAST else 1
-            w = NT // halves
-            for i in range(halves):
-                part_cols = slice(NT * n + w * i, NT * n + w * (i + 1))
-                nc.vector.tensor_tensor(res[:, m, part_cols], y[:, w * i : w * (i + 1)], res[:, m, part_cols], ADD)
-                if m == MT - 1:
-                    nc.scalar.dma_start(out=out[P * m : P * (m + 1), part_cols], in_=res[:, m, part_cols])
-            if m < MT - 1 and n == LAST:
-                nc.scalar.dma_start(out=out[P * m : P * (m + 1), :], in_=res[:, m, :])
+                    w4_pass(ys[m, n][:], a, m, n)
+            up_pass(ys[m, n][:], m, n)
+            add_prev(ys[m, n][:], m, NT * n, NT)
+            if m == MT - 1:
+                store(m, NT * n, NT)
+            elif n == LAST:
+                store(m, 0, S)
+        m, n = order[-1]
+        for strips in ((0, 1), (2,), (3,)):
+            bank = open_bank()
+            for i, b in enumerate(strips):
+                for a in range(PASSES):
+                    w4_pass(bank[:, P * i : P * (i + 1)], a, m, n, P * b, P * (b + 1), i == 0)
+                up_pass(bank[:, P * i : P * (i + 1)], m, n, P * b, P * (b + 1), i == len(strips) - 1)
+            add_prev(bank[:, 0 : P * len(strips)], m, NT * n + P * strips[0], P * len(strips))
+            if strips == (2,):
+                store(m, NT * n, 3 * P)
+        store(m, NT * n + 3 * P, P)

@@ -64,9 +64,14 @@ def tile_list_tablora_res_kernel(
 
         raw, win_w = {}, {}
 
-        def load_down(a):
-            raw[a] = staged(f"raw{a}", [P, 4, R], F32, (14, 24, 14)[a])
-            nc.sync.dma_start(out=raw[a][:], in_=down[512 * a : 512 * (a + 1), :].rearrange("(p j) w -> p j w", j=4))
+        def load_down(a0, a1):
+            rows_of_down = staged(f"raw{a0}", [P, a1 - a0, 4, R], F32, 14)
+            nc.sync.dma_start(
+                out=rows_of_down[:].rearrange("p a j w -> p a (j w)"),
+                in_=down[512 * a0 : 512 * a1, :].rearrange("(a p j) w -> p a (j w)", p=P, j=4),
+            )
+            for a in range(a0, a1):
+                raw[a] = rows_of_down[:, a - a0, :, :]
 
         def load_words(a):
             win_w[a] = staged(f"win_w{a}", [P, T], I32, (80, 64, 82)[a])
@@ -95,8 +100,7 @@ def tile_list_tablora_res_kernel(
             for m in range(m0, m1):
                 w4_planes[m] = (scales, m - m0)
 
-        load_down(0)
-        load_down(1)
+        load_down(0, 2)
         load_words(0)
 
         planes = [staged(f"plane{a}", [P, S], U8, 154 + 1.5 * a, MOVING_SCALES) for a in range(PASSES)]
@@ -126,7 +130,7 @@ def tile_list_tablora_res_kernel(
             else:
                 grp = grps.tile([P, 4 * R], BF16, name="grp", align_bytes=64)
             dst = grp[:].rearrange("p (t m j) -> p m t j", t=4, j=4)
-            src = raw[a][:].rearrange("p j (m t) -> p m t j", t=4)
+            src = raw[a].rearrange("p j (m t) -> p m t j", t=4)
             if a < PASSES - 1:
                 nc.scalar.copy(out=dst, in_=src)
             else:
@@ -185,7 +189,8 @@ def tile_list_tablora_res_kernel(
         first = parked + kept[: 8 - len(parked)]
 
         quantize_down(0)
-        load_down(2)
+        quantize_down(1)
+        load_down(2, 3)
         load_w4_words("w4_first_words", 0, 1, 152)
         load_w4_scales(first_scales, 0, 1)
         banks = {}
@@ -196,7 +201,6 @@ def tile_list_tablora_res_kernel(
         for n, b in first:
             banks[n, b] = open_bank()
             h_passes(banks[n, b], 0, n, b, True, False)
-        quantize_down(1)
         for n in (2, 1, 0):
             gather_words(1, n)
         load_w4_words("w4_rest_words", 1, MT, 64)
@@ -226,8 +230,10 @@ def tile_list_tablora_res_kernel(
         load_w4_scales(rest_scales, 1, MT)
         nc.sync.dma_start(out=up_raw[:, 2:4, :], in_=up_rows[:, 2:4, :])
         res = staged("res", [P, MT, S], F32, 16)
-        for m in range(MT):
-            nc.sync.dma_start(out=res[:, m, :], in_=prev[P * m : P * (m + 1), :])
+        for m0, m1 in ((0, 2), (2, 4), (4, 6), (6, 7), (7, 8)):
+            nc.sync.dma_start(
+                out=res[:, m0:m1, :], in_=prev[P * m0 : P * m1, :].rearrange("(m p) s -> p m s", p=P)
+            )
         for n in range(CHUNKS):
             gather_words(2, n)
         ucodes, uscales = {}, {}
@@ -309,7 +315,9 @@ def tile_list_tablora_res_kernel(
             add_prev(ys[m, n][:], m, NT * n, NT)
             if m == MT - 1:
                 store(m, NT * n, NT)
-            elif n == LAST:
+            elif (m, n) == (1, LAST):
+                nc.scalar.dma_start(out=out[0 : 2 * P, :].rearrange("(m p) s -> p m s", p=P), in_=res[:, 0:2, :])
+            elif m > 1 and n == LAST:
                 store(m, 0, S)
         m, n = order[-1]
         for strips in ((0, 1), (2,), (3,)):

@@ -28,6 +28,7 @@ KB = 1024
 FIRST_SCALE_ROW = 48
 KEPT = 5
 MOVING_CODES, MOVING_SCALES = 192, 64
+STORE_FROM = {3: 0, 5: 4, 6: 6}
 
 
 def tile_list_tablora_res_kernel(
@@ -55,8 +56,8 @@ def tile_list_tablora_res_kernel(
 
         win_s = staged("win_s", [P, T // 4], I32, 62)
         rows = tab[:, 512 * T : 528 * T].rearrange("a (q t) -> a q t", q=16).bitcast(I32)
-        for a in range(PASSES):
-            nc.sync.dma_start(out=win_s[FIRST_SCALE_ROW + a : FIRST_SCALE_ROW + 48 : PASSES, :], in_=rows[a])
+        nc.sync.dma_start(out=win_s[64:96, :], in_=rows[0:2].rearrange("a q t -> q a t"))
+        nc.sync.dma_start(out=win_s[FIRST_SCALE_ROW:64, :], in_=rows[2])
         nc.vector.memset(win_s[0:FIRST_SCALE_ROW, :], 0)
         nc.vector.memset(win_s[FIRST_SCALE_ROW + 48 : P, :], 0)
         offsets = lists.tile([P, S // 16], U16, name="offsets")
@@ -103,24 +104,24 @@ def tile_list_tablora_res_kernel(
         load_down(0, 2)
         load_words(0)
 
-        planes = [staged(f"plane{a}", [P, S], U8, 154 + 1.5 * a, MOVING_SCALES) for a in range(PASSES)]
-        for plane in planes:
+        early_planes = staged("early_planes", [P, 2 * S], U8, 154, MOVING_SCALES)
+        last_plane = staged("last_plane", [P, S], U8, 157, MOVING_SCALES)
+        for plane in (early_planes, last_plane):
             nc.vector.memset(plane[:].bitcast(I32), 0)
+        planes = [early_planes[:, 0:S], early_planes[:, S : 2 * S], last_plane[:]]
 
         gs = keep.tile([P, S], U8, name="gs", align_bytes=64)
         nc.vector.tensor_copy(gs[:], win_s[:].bitcast(U8).indirect(offsets[:]))
 
-        def move_plane(a, queue):
+        def move_rows(plane, first, count):
             for q in range(4):
-                first = FIRST_SCALE_ROW + 4 * PASSES * q
-                queue.dma_start(
-                    out=planes[a][32 * q : 32 * q + 4, :].bitcast(I32),
-                    in_=gs[first + a : first + 4 * PASSES : PASSES, :].bitcast(I32),
+                nc.sync.dma_start(
+                    out=plane[32 * q : 32 * q + 4, :].bitcast(I32),
+                    in_=gs[first + count * q : first + count * (q + 1), :].bitcast(I32),
                 )
 
-        move_plane(0, nc.sync)
+        move_rows(early_planes, 64, 8)
         load_words(1)
-        move_plane(1, nc.sync)
 
         dcodes, dscales = [], []
 
@@ -142,13 +143,15 @@ def tile_list_tablora_res_kernel(
             dscales.append(s)
 
         gw = {}
-        OC = NT // 16
-
-        def gather_words(a, n):
+        def gather_words(a, n, pieces=1):
             t = staged(f"gw{a}_{n}", [P, NT], U32, 116 + 2 * (CHUNKS * a + n), MOVING_CODES)
-            nc.vector.tensor_copy(
-                t[:], win_w[a][:].bitcast(U32).indirect(offsets[:, OC * n : OC * (n + 1)])
-            )
+            width = NT // pieces
+            for i in range(pieces):
+                first = (NT * n + width * i) // 16
+                nc.vector.tensor_copy(
+                    t[:, width * i : width * (i + 1)],
+                    win_w[a][:].bitcast(U32).indirect(offsets[:, first : first + width // 16]),
+                )
             gw[a, n] = t
 
         def open_bank():
@@ -197,7 +200,7 @@ def tile_list_tablora_res_kernel(
         for n in (1, 2, 0):
             gather_words(0, n)
         load_words(2)
-        move_plane(2, nc.sync)
+        move_rows(last_plane, FIRST_SCALE_ROW, 4)
         for n, b in first:
             banks[n, b] = open_bank()
             h_passes(banks[n, b], 0, n, b, True, False)
@@ -226,16 +229,15 @@ def tile_list_tablora_res_kernel(
         quantize_down(2)
         up_raw = staged("up_raw", [P, 4, M], F32, 0)
         up_rows = up.rearrange("(p j) w -> p j w", j=4)
-        nc.sync.dma_start(out=up_raw[:, 0:2, :], in_=up_rows[:, 0:2, :])
         load_w4_scales(rest_scales, 1, MT)
-        nc.sync.dma_start(out=up_raw[:, 2:4, :], in_=up_rows[:, 2:4, :])
+        nc.sync.dma_start(out=up_raw[:], in_=up_rows)
         res = staged("res", [P, MT, S], F32, 16)
-        for m0, m1 in ((0, 2), (2, 4), (4, 6), (6, 7), (7, 8)):
+        for m0, m1 in ((0, 2), (2, 4), (4, 8)):
             nc.sync.dma_start(
                 out=res[:, m0:m1, :], in_=prev[P * m0 : P * m1, :].rearrange("(m p) s -> p m s", p=P)
             )
         for n in range(CHUNKS):
-            gather_words(2, n)
+            gather_words(2, n, 2 if n == 0 else 1)
         ucodes, uscales = {}, {}
 
         def quantize_up(i):
@@ -302,7 +304,12 @@ def tile_list_tablora_res_kernel(
 
         def store(m, first, width):
             cols = slice(first, first + width)
-            nc.scalar.dma_start(out=out[P * m : P * (m + 1), cols], in_=res[:, m, cols])
+            nc.sync.dma_start(out=out[P * m : P * (m + 1), cols], in_=res[:, m, cols])
+
+        def store_rows(m0, m1):
+            nc.sync.dma_start(
+                out=out[P * m0 : P * m1, :].rearrange("(m p) s -> p m s", p=P), in_=res[:, m0:m1, :]
+            )
 
         for m, n in order[:-1]:
             if (m, n) in ((2, 0), (4, 0)):
@@ -315,18 +322,15 @@ def tile_list_tablora_res_kernel(
             add_prev(ys[m, n][:], m, NT * n, NT)
             if m == MT - 1:
                 store(m, NT * n, NT)
-            elif (m, n) == (1, LAST):
-                nc.scalar.dma_start(out=out[0 : 2 * P, :].rearrange("(m p) s -> p m s", p=P), in_=res[:, 0:2, :])
-            elif m > 1 and n == LAST:
-                store(m, 0, S)
+            elif n == LAST and m in STORE_FROM:
+                store_rows(STORE_FROM[m], m + 1)
         m, n = order[-1]
-        for strips in ((0, 1), (2,), (3,)):
+        for c0, c1 in ((0, 2 * P), (2 * P, 3 * P), (3 * P, NT)):
             bank = open_bank()
-            for i, b in enumerate(strips):
-                for a in range(PASSES):
-                    w4_pass(bank[:, P * i : P * (i + 1)], a, m, n, P * b, P * (b + 1), i == 0)
-                up_pass(bank[:, P * i : P * (i + 1)], m, n, P * b, P * (b + 1), i == len(strips) - 1)
-            add_prev(bank[:, 0 : P * len(strips)], m, NT * n + P * strips[0], P * len(strips))
-            if strips == (2,):
+            for a in range(PASSES):
+                w4_pass(bank[:, 0 : c1 - c0], a, m, n, c0, c1)
+            up_pass(bank[:, 0 : c1 - c0], m, n, c0, c1)
+            add_prev(bank[:, 0 : c1 - c0], m, NT * n + c0, c1 - c0)
+            if c1 == 3 * P:
                 store(m, NT * n, 3 * P)
         store(m, NT * n + 3 * P, P)

@@ -28,6 +28,7 @@ KB = 1024
 FIRST_SCALE_ROW = 48
 KEPT = 5
 MOVING_CODES, MOVING_SCALES = 192, 64
+QUADRANTS = (0, 2, 1, 3)
 STORE_FROM = {3: 0, 5: 4, 6: 6}
 
 
@@ -93,7 +94,7 @@ def tile_list_tablora_res_kernel(
 
         def load_w4_scales(scales, m0, m1):
             scale_rows = w4_scales[:, :, P * m0 : P * m1].bitcast(I32)
-            for q in range(4):
+            for q in QUADRANTS:
                 nc.sync.dma_start(
                     out=scales[32 * q : 32 * q + 4, :, :].bitcast(I32),
                     in_=scale_rows[:, 4 * q : 4 * q + 4, :].rearrange("a r n -> r a n"),
@@ -114,7 +115,7 @@ def tile_list_tablora_res_kernel(
         nc.vector.tensor_copy(gs[:], win_s[:].bitcast(U8).indirect(offsets[:]))
 
         def move_rows(plane, first, count):
-            for q in range(4):
+            for q in QUADRANTS:
                 nc.sync.dma_start(
                     out=plane[32 * q : 32 * q + 4, :].bitcast(I32),
                     in_=gs[first + count * q : first + count * (q + 1), :].bitcast(I32),
@@ -143,10 +144,10 @@ def tile_list_tablora_res_kernel(
             dscales.append(s)
 
         gw = {}
-        def gather_words(a, n, pieces=1):
+        def gather_words(a, n, pieces=(0,)):
             t = staged(f"gw{a}_{n}", [P, NT], U32, 116 + 2 * (CHUNKS * a + n), MOVING_CODES)
-            width = NT // pieces
-            for i in range(pieces):
+            width = NT // len(pieces)
+            for i in pieces:
                 first = (NT * n + width * i) // 16
                 nc.vector.tensor_copy(
                     t[:, width * i : width * (i + 1)],
@@ -184,7 +185,7 @@ def tile_list_tablora_res_kernel(
             )
 
         def interleaved(bank):
-            return bank[:].rearrange("p (t c) -> p c t", t=RT)
+            return bank[:].rearrange("p (t c i) -> p c t i", t=RT, i=2)
 
         blocks = [(n, b) for n in range(CHUNKS) for b in range(4)]
         kept, parked = blocks[:KEPT], blocks[KEPT:][::-1]
@@ -197,7 +198,7 @@ def tile_list_tablora_res_kernel(
         load_w4_words("w4_first_words", 0, 1, 152)
         load_w4_scales(first_scales, 0, 1)
         banks = {}
-        for n in (1, 2, 0):
+        for n in (2, 1, 0):
             gather_words(0, n)
         load_words(2)
         move_rows(last_plane, FIRST_SCALE_ROW, 4)
@@ -205,16 +206,16 @@ def tile_list_tablora_res_kernel(
             banks[n, b] = open_bank()
             h_passes(banks[n, b], 0, n, b, True, False)
         for n in (2, 1, 0):
-            gather_words(1, n)
+            gather_words(1, n, (1, 0) if n == LAST else (0,))
         load_w4_words("w4_rest_words", 1, MT, 64)
         rest_scales = zeroed_w4_scales("w4_rest_scales", MT - 1, 70)
         part = {}
         for n, b in parked:
             h_passes(banks[n, b], 1, n, b, False, True)
             if n == LAST and b >= 2:
-                part[n, b] = staged(f"part{n}_{b}", [P, P, 4], F32, 100 + 2 * b)
+                part[n, b] = staged(f"part{n}_{b}", [P, P // 2, 4, 2], F32, 100 + 2 * b)
             else:
-                part[n, b] = keep.tile([P, P, 4], F32, name=f"part{n}_{b}")
+                part[n, b] = keep.tile([P, P // 2, 4, 2], F32, name=f"part{n}_{b}")
             nc.scalar.copy(out=part[n, b][:], in_=interleaved(banks[n, b]))
         for n, b in kept[::-1]:
             if (n, b) not in first:
@@ -237,7 +238,7 @@ def tile_list_tablora_res_kernel(
                 out=res[:, m0:m1, :], in_=prev[P * m0 : P * m1, :].rearrange("(m p) s -> p m s", p=P)
             )
         for n in range(CHUNKS):
-            gather_words(2, n, 2 if n == 0 else 1)
+            gather_words(2, n, (0, 1) if n == 0 else (0,))
         ucodes, uscales = {}, {}
 
         def quantize_up(i):
@@ -262,7 +263,7 @@ def tile_list_tablora_res_kernel(
         for n in range(CHUNKS):
             h_grp[n] = grps.tile([P, 4 * R], BF16, name="grp", align_bytes=64)
             for b in range(4):
-                dst = h_grp[n][:, 512 * b : 512 * (b + 1)].rearrange("p (c t) -> p c t", t=4)
+                dst = h_grp[n][:, 512 * b : 512 * (b + 1)].rearrange("p (c i t) -> p c t i", t=4, i=2)
                 if (n, b) in kept:
                     h_passes(banks[n, b], 2, n, b, False, True)
                     nc.scalar.copy(out=dst, in_=interleaved(banks[n, b]))

@@ -230,8 +230,9 @@ def tile_list_tablora_res_kernel(
         quantize_down(2)
         up_raw = staged("up_raw", [P, 4, M], F32, 0)
         up_rows = up.rearrange("(p j) w -> p j w", j=4)
+        nc.sync.dma_start(out=up_raw[:, 0:1, :], in_=up_rows[:, 0:1, :])
         load_w4_scales(rest_scales, 1, MT)
-        nc.sync.dma_start(out=up_raw[:], in_=up_rows)
+        nc.sync.dma_start(out=up_raw[:, 1:4, :], in_=up_rows[:, 1:4, :])
         res = staged("res", [P, MT, S], F32, 16)
         for m0, m1 in ((0, 2), (2, 4), (4, 8)):
             nc.sync.dma_start(
@@ -303,12 +304,14 @@ def tile_list_tablora_res_kernel(
             cols = slice(first, first + width)
             nc.vector.tensor_tensor(res[:, m, cols], bank, res[:, m, cols], ADD)
 
+        queues = [nc.sync, nc.scalar] * 4
+
         def store(m, first, width):
             cols = slice(first, first + width)
-            nc.sync.dma_start(out=out[P * m : P * (m + 1), cols], in_=res[:, m, cols])
+            queues.pop(0).dma_start(out=out[P * m : P * (m + 1), cols], in_=res[:, m, cols])
 
         def store_rows(m0, m1):
-            nc.sync.dma_start(
+            queues.pop(0).dma_start(
                 out=out[P * m0 : P * m1, :].rearrange("(m p) s -> p m s", p=P), in_=res[:, m0:m1, :]
             )
 

@@ -29,7 +29,7 @@ FIRST_SCALE_ROW = 48
 KEPT = 5
 MOVING_CODES, MOVING_SCALES = 192, 64
 QUADRANTS = (0, 2, 1, 3)
-STORE_FROM = {3: 0, 5: 4, 6: 6}
+STORE_FROM = {3: 0, 5: 4}
 
 
 def tile_list_tablora_res_kernel(
@@ -304,7 +304,7 @@ def tile_list_tablora_res_kernel(
             cols = slice(first, first + width)
             nc.vector.tensor_tensor(res[:, m, cols], bank, res[:, m, cols], ADD)
 
-        queues = [nc.sync, nc.scalar] * 4
+        queues = [nc.sync, nc.scalar] * 5
 
         def store(m, first, width):
             cols = slice(first, first + width)
@@ -323,8 +323,15 @@ def tile_list_tablora_res_kernel(
                 for a in range(PASSES):
                     w4_pass(ys[m, n][:], a, m, n)
             up_pass(ys[m, n][:], m, n)
+            if (m, n) == order[-2]:
+                for c0 in (0, NT // 2):
+                    add_prev(ys[m, n][:, c0 : c0 + NT // 2], m, NT * n + c0, NT // 2)
+                    store(m, NT * n + c0, NT // 2)
+                continue
             add_prev(ys[m, n][:], m, NT * n, NT)
-            if m == MT - 1:
+            if (m, n) == (MT - 2, 1):
+                store(m, 0, 2 * NT)
+            elif (m, n) > (MT - 2, 1):
                 store(m, NT * n, NT)
             elif n == LAST and m in STORE_FROM:
                 store_rows(STORE_FROM[m], m + 1)

from contextlib import ExitStack

import concourse.mybir as mybir

K, R, M, T, S = 1536, 512, 1024, 4096, 1536

FLOPS = 2 * S * (K * R + K * M + R * M)

F32 = mybir.dt.float32
BF16 = mybir.dt.bfloat16
I32 = mybir.dt.int32
U32 = mybir.dt.uint32
U16 = mybir.dt.uint16
U8 = mybir.dt.uint8
FP8X4 = mybir.dt.float8_e4m3fn_x4
FP4X4 = mybir.dt.float4_e2m1fn_x4
ADD = mybir.AluOpType.add

P = 128
PASSES = K // 512
NT = 512
CHUNKS = S // NT
RT = R // P
MT = M // P


KB = 1024
FIRST_SCALE_ROW = 48
KEPT = 5
MOVING_CODES, MOVING_SCALES = 192, 64
QUADRANTS = (0, 2, 1, 3)
STORE_FROM = {3: 0, 5: 4}


def tile_list_tablora_res_kernel(
    tc, tab, w4_words, w4_scales, down, up, prev, offs, out
):
    nc = tc.nc
    with ExitStack() as ctx:
        lists = ctx.enter_context(tc.tile_pool(name="lists", bufs=1))
        keep = ctx.enter_context(tc.tile_pool(name="keep", bufs=1))
        stage = ctx.enter_context(tc.tile_pool(name="stage", bufs=1))
        grps = ctx.enter_context(tc.tile_pool(name="grps", bufs=3))
        psum = ctx.enter_context(tc.psum_pool(name="psum", bufs=8))

        def staged(name, shape, dtype, kb, phase=0):
            return stage.tile(
                shape, dtype, name=name, offset=int(kb * KB) + phase, align_bytes=64 if phase else 256
            )

        def zeroed_w4_scales(name, tiles, kb):
            scales = staged(name, [P, PASSES, P * tiles], U8, kb)
            nc.vector.memset(scales[:].rearrange("p a n -> p (a n)").bitcast(I32), 0)
            return scales

        first_scales = zeroed_w4_scales("w4_first_scales", 1, 160)

        win_s = staged("win_s", [P, T // 4], I32, 62)
        rows = tab[:, 512 * T : 528 * T].rearrange("a (q t) -> a q t", q=16).bitcast(I32)
        nc.sync.dma_start(out=win_s[64:96, :], in_=rows[0:2].rearrange("a q t -> q a t"))
        nc.sync.dma_start(out=win_s[FIRST_SCALE_ROW:64, :], in_=rows[2])
        nc.vector.memset(win_s[0:FIRST_SCALE_ROW, :], 0)
        nc.vector.memset(win_s[FIRST_SCALE_ROW + 48 : P, :], 0)
        offsets = lists.tile([P, S // 16], U16, name="offsets")
        nc.sync.dma_start(offsets[:], offs)

        raw, win_w = {}, {}

        def load_down(a0, a1):
            rows_of_down = staged(f"raw{a0}", [P, a1 - a0, 4, R], F32, 14)
            nc.sync.dma_start(
                out=rows_of_down[:].rearrange("p a j w -> p a (j w)"),
                in_=down[512 * a0 : 512 * a1, :].rearrange("(a p j) w -> p a (j w)", p=P, j=4),
            )
            for a in range(a0, a1):
                raw[a] = rows_of_down[:, a - a0, :, :]

        def load_words(a):
            win_w[a] = staged(f"win_w{a}", [P, T], I32, (80, 64, 82)[a])
            nc.sync.dma_start(
                out=win_w[a][:], in_=tab[a, 0 : 512 * T].rearrange("(p b) -> p b", p=P).bitcast(I32)
            )

        w4_codes, w4_planes = {}, {}

        def load_w4_words(name, m0, m1, kb):
            words = staged(name, [P, PASSES, 2 * P * (m1 - m0)], U8, kb)
            nc.sync.dma_start(
                out=words[:].bitcast(I32),
                in_=w4_words[:, :, 2 * P * m0 : 2 * P * m1].bitcast(I32).rearrange("a p b -> p a b"),
            )
            for m in range(m0, m1):
                w4_codes[m] = (words, m - m0)

        def load_w4_scales(scales, m0, m1):
            scale_rows = w4_scales[:, :, P * m0 : P * m1].bitcast(I32)
            for q in QUADRANTS:
                nc.sync.dma_start(
                    out=scales[32 * q : 32 * q + 4, :, :].bitcast(I32),
                    in_=scale_rows[:, 4 * q : 4 * q + 4, :].rearrange("a r n -> r a n"),
                )
            for m in range(m0, m1):
                w4_planes[m] = (scales, m - m0)

        load_down(0, 2)
        load_words(0)

        early_planes = staged("early_planes", [P, 2 * S], U8, 154, MOVING_SCALES)
        last_plane = staged("last_plane", [P, S], U8, 157, MOVING_SCALES)
        for plane in (early_planes, last_plane):
            nc.vector.memset(plane[:].bitcast(I32), 0)
        planes = [early_planes[:, 0:S], early_planes[:, S : 2 * S], last_plane[:]]

        gs = keep.tile([P, S], U8, name="gs", align_bytes=64)
        nc.vector.tensor_copy(gs[:], win_s[:].bitcast(U8).indirect(offsets[:]))

        def move_rows(plane, first, count):
            for q in QUADRANTS:
                nc.sync.dma_start(
                    out=plane[32 * q : 32 * q + 4, :].bitcast(I32),
                    in_=gs[first + count * q : first + count * (q + 1), :].bitcast(I32),
                )

        move_rows(early_planes, 64, 8)
        load_words(1)

        dcodes, dscales = [], []

        def quantize_down(a):
            if a == 0:
                grp = staged("grp0", [P, 4 * R], BF16, 98)
            else:
                grp = grps.tile([P, 4 * R], BF16, name="grp", align_bytes=64)
            dst = grp[:].rearrange("p (t m j) -> p m t j", t=4, j=4)
            src = raw[a].rearrange("p j (m t) -> p m t j", t=4)
            if a < PASSES - 1:
                nc.scalar.copy(out=dst, in_=src)
            else:
                nc.vector.tensor_copy(out=dst, in_=src)
            c = staged(f"dcodes{a}", [P, R], U32, 142 + 2 * a)
            s = staged(f"dscales{a}", [P, R], U8, 148 + 0.5 * a)
            nc.vector.quantize_mx(out=c[:].bitcast(FP8X4), scales=s[:], in_=grp[:])
            dcodes.append(c)
            dscales.append(s)

        gw = {}
        def gather_words(a, n, pieces=(0,)):
            t = staged(f"gw{a}_{n}", [P, NT], U32, 116 + 2 * (CHUNKS * a + n), MOVING_CODES)
            width = NT // len(pieces)
            for i in pieces:
                first = (NT * n + width * i) // 16
                nc.vector.tensor_copy(
                    t[:, width * i : width * (i + 1)],
                    win_w[a][:].bitcast(U32).indirect(offsets[:, first : first + width // 16]),
                )
            gw[a, n] = t

        def open_bank():
            return psum.tile([P, NT], F32, name="bank")

        LAST = CHUNKS - 1

        def h_passes(bank, a, n, b, start, stop):
            for t in range(RT):
                nc.tensor.matmul_mx(
                    out=bank[:, P * t : P * (t + 1)],
                    lhsT=dcodes[a][:, P * t : P * (t + 1)].bitcast(FP8X4),
                    lhsT_scale=dscales[a][:, P * t : P * (t + 1)],
                    rhs=gw[a, n][:, P * b : P * (b + 1)].bitcast(FP8X4),
                    rhs_scale=planes[a][:, NT * n + P * b : NT * n + P * (b + 1)],
                    start=start and t == 0,
                    stop=stop and t == RT - 1,
                )

        def w4_pass(bank, a, m, n, c0=0, c1=NT, start=True):
            (words, i), (scales, j) = w4_codes[m], w4_planes[m]
            nc.tensor.matmul_mx(
                out=bank,
                lhsT=words[:, a, 2 * P * i : 2 * P * (i + 1)].bitcast(FP4X4),
                lhsT_scale=scales[:, a, P * j : P * (j + 1)],
                rhs=gw[a, n][:, c0:c1].bitcast(FP8X4),
                rhs_scale=planes[a][:, NT * n + c0 : NT * n + c1],
                start=(a == 0 and start),
                stop=False,
            )

        def interleaved(bank):
            return bank[:].rearrange("p (t c i) -> p c t i", t=RT, i=2)

        blocks = [(n, b) for n in range(CHUNKS) for b in range(4)]
        kept, parked = blocks[:KEPT], blocks[KEPT:][::-1]
        early = [(i // CHUNKS, i % CHUNKS) for i in range(8 - KEPT)]
        first = parked + kept[: 8 - len(parked)]

        quantize_down(0)
        quantize_down(1)
        load_down(2, 3)
        load_w4_words("w4_first_words", 0, 1, 152)
        load_w4_scales(first_scales, 0, 1)
        banks = {}
        for n in (2, 1, 0):
            gather_words(0, n)
        load_words(2)
        move_rows(last_plane, FIRST_SCALE_ROW, 4)
        for n, b in first:
            banks[n, b] = open_bank()
            h_passes(banks[n, b], 0, n, b, True, False)
        for n in (2, 1, 0):
            gather_words(1, n, (1, 0) if n == LAST else (0,))
        load_w4_words("w4_rest_words", 1, MT, 64)
        rest_scales = zeroed_w4_scales("w4_rest_scales", MT - 1, 70)
        part = {}
        for n, b in parked:
            h_passes(banks[n, b], 1, n, b, False, True)
            if n == LAST and b >= 2:
                part[n, b] = staged(f"part{n}_{b}", [P, P // 2, 4, 2], F32, 100 + 2 * b)
            else:
                part[n, b] = keep.tile([P, P // 2, 4, 2], F32, name=f"part{n}_{b}")
            nc.scalar.copy(out=part[n, b][:], in_=interleaved(banks[n, b]))
        for n, b in kept[::-1]:
            if (n, b) not in first:
                banks[n, b] = open_bank()
                h_passes(banks[n, b], 0, n, b, True, False)
            h_passes(banks[n, b], 1, n, b, False, False)
        ys = {}
        for m, n in early:
            ys[m, n] = open_bank()
            for a in range(PASSES - 1):
                w4_pass(ys[m, n][:], a, m, n)
        quantize_down(2)
        up_raw = staged("up_raw", [P, 4, M], F32, 0)
        up_rows = up.rearrange("(p j) w -> p j w", j=4)
        nc.sync.dma_start(out=up_raw[:, 0:1, :], in_=up_rows[:, 0:1, :])
        load_w4_scales(rest_scales, 1, MT)
        nc.sync.dma_start(out=up_raw[:, 1:4, :], in_=up_rows[:, 1:4, :])
        res = staged("res", [P, MT, S], F32, 16)
        for m0, m1 in ((0, 2), (2, 4), (4, 8)):
            nc.sync.dma_start(
                out=res[:, m0:m1, :], in_=prev[P * m0 : P * m1, :].rearrange("(m p) s -> p m s", p=P)
            )
        for n in range(CHUNKS):
            gather_words(2, n, (0, 1) if n == 0 else (0,))
        ucodes, uscales = {}, {}

        def quantize_up(i):
            cols = slice(256 * i, 256 * (i + 1))
            if i == 0:
                up_grp = staged("up_grp0", [P, 256, 4], BF16, 109)
            else:
                up_grp = keep.tile([P, 256, 4], BF16, name=f"up_grp{i}", align_bytes=64)
            nc.scalar.copy(
                out=up_grp[:].rearrange("p (c i) j -> p c j i", i=4),
                in_=up_raw[:, :, cols].rearrange("p j (c i) -> p c j i", i=4),
            )
            ucodes[i] = staged(f"ucodes{i}", [P, 256], U32, (112, 113, 114, 113)[i])
            uscales[i] = staged(f"uscales{i}", [P, 256], U8, 141 + 0.25 * i)
            nc.vector.quantize_mx(
                out=ucodes[i][:].bitcast(FP8X4),
                scales=uscales[i][:],
                in_=up_grp[:].rearrange("p c j -> p (c j)"),
            )

        h_grp = {}
        for n in range(CHUNKS):
            h_grp[n] = grps.tile([P, 4 * R], BF16, name="grp", align_bytes=64)
            for b in range(4):
                dst = h_grp[n][:, 512 * b : 512 * (b + 1)].rearrange("p (c i t) -> p c t i", t=4, i=2)
                if (n, b) in kept:
                    h_passes(banks[n, b], 2, n, b, False, True)
                    nc.scalar.copy(out=dst, in_=interleaved(banks[n, b]))
                else:
                    bank = open_bank()
                    h_passes(bank, 2, n, b, True, True)
                    nc.vector.tensor_tensor(dst, interleaved(bank), part[n, b][:], ADD)
            for m in range(2):
                if (m, n) in ys:
                    w4_pass(ys[m, n][:], PASSES - 1, m, n)
        hcodes, hscales = {}, {}
        for n in range(CHUNKS):
            if n == 1:
                quantize_up(0)
            hcodes[n] = staged(f"hcodes{n}", [P, NT], U32, (105, 107.5, 109.5)[n], MOVING_CODES)
            hscales[n] = staged(f"hscales{n}", [P, NT], U8, 139 + 0.5 * n, MOVING_SCALES)
            nc.vector.quantize_mx(out=hcodes[n][:].bitcast(FP8X4), scales=hscales[n][:], in_=h_grp[n][:])
        quantize_up(1)

        half = 2
        order = [(m, n) for n in range(CHUNKS) for m in range(half)]
        order += [(m, n) for m in range(half, MT) for n in range(CHUNKS)]

        def up_pass(bank, m, n, c0=0, c1=NT, stop=True):
            ucols = slice(P * (m % 2), P * (m % 2 + 1))
            nc.tensor.matmul_mx(
                out=bank,
                lhsT=ucodes[m // 2][:, ucols].bitcast(FP8X4),
                lhsT_scale=uscales[m // 2][:, ucols],
                rhs=hcodes[n][:, c0:c1].bitcast(FP8X4),
                rhs_scale=hscales[n][:, c0:c1],
                start=False,
                stop=stop,
            )

        def add_prev(bank, m, first, width):
            cols = slice(first, first + width)
            nc.vector.tensor_tensor(res[:, m, cols], bank, res[:, m, cols], ADD)

        queues = [nc.sync, nc.scalar] * 5

        def store(m, first, width):
            cols = slice(first, first + width)
            queues.pop(0).dma_start(out=out[P * m : P * (m + 1), cols], in_=res[:, m, cols])

        def store_rows(m0, m1):
            queues.pop(0).dma_start(
                out=out[P * m0 : P * m1, :].rearrange("(m p) s -> p m s", p=P), in_=res[:, m0:m1, :]
            )

        for m, n in order[:-1]:
            if (m, n) in ((2, 0), (4, 0)):
                quantize_up(m // 2 + 1)
            if (m, n) not in ys:
                ys[m, n] = open_bank()
                for a in range(PASSES):
                    w4_pass(ys[m, n][:], a, m, n)
            up_pass(ys[m, n][:], m, n)
            if (m, n) == order[-2]:
                for c0 in (0, NT // 2):
                    add_prev(ys[m, n][:, c0 : c0 + NT // 2], m, NT * n + c0, NT // 2)
                    store(m, NT * n + c0, NT // 2)
                continue
            add_prev(ys[m, n][:], m, NT * n, NT)
            if (m, n) == (MT - 2, 1):
                store(m, 0, 2 * NT)
            elif (m, n) > (MT - 2, 1):
                store(m, NT * n, NT)
            elif n == LAST and m in STORE_FROM:
                store_rows(STORE_FROM[m], m + 1)
        m, n = order[-1]
        for c0, c1 in ((0, 2 * P), (2 * P, 3 * P), (3 * P, NT)):
            bank = open_bank()
            for a in range(PASSES):
                w4_pass(bank[:, 0 : c1 - c0], a, m, n, c0, c1)
            up_pass(bank[:, 0 : c1 - c0], m, n, c0, c1)
            add_prev(bank[:, 0 : c1 - c0], m, NT * n + c0, c1 - c0)
            if c1 == 3 * P:
                store(m, NT * n, 3 * P)
        store(m, NT * n + 3 * P, P)
